import numpy as np
import ml_dtypes


def mxq(x, axis, fmt="e4m3"):
    dtype, down = {"e4m3": (ml_dtypes.float8_e4m3fn, 7), "e5m2": (ml_dtypes.float8_e5m2, 14)}[fmt]
    v = np.moveaxis(np.asarray(x, np.float32).astype(ml_dtypes.bfloat16).astype(np.float64), axis, -1)
    blocks = v.reshape(v.shape[:-1] + (-1, 32))
    amax = np.abs(blocks).max(-1, keepdims=True)
    byte = np.maximum(np.where(amax > 0, np.frexp(amax)[1] - 1 + 127, 0) - down, 1)
    scale = np.exp2(byte - 127.0)
    codes = (blocks / scale).astype(np.float32).astype(dtype).astype(np.float64)
    return np.moveaxis((codes * scale).reshape(v.shape), -1, axis)


WIDE = False


def mx_kscale(k):
    if not WIDE:
        return np.ones(k)
    levels = np.array([10, -10, 5, -5, 0])
    if k % 512:
        return np.exp2(np.random.permutation(np.resize(levels, k // 32))).repeat(32)
    a = np.empty((k // 512, 16))
    for p in range(k // 512):
        a[p, :8] = np.random.permutation(np.resize(levels, 8))
        for g in range(8):
            far = levels[np.abs(levels - a[p, g]) >= 10]
            a[p, g + 8] = far[np.random.randint(len(far))]
    return np.exp2(a.ravel()).repeat(32)


def f64(x):
    return np.asarray(x).astype(np.float64)


def striped(idx):
    return np.tile(idx.reshape(-1, 16).T, (8, 1)).astype(np.uint16)


def unstriped(offs):
    return offs[:16].T.reshape(-1).astype(np.int64)


E2M1 = np.array([0.0, 0.5, 1.0, 1.5, 2.0, 3.0, 4.0, 6.0, -0.0, -0.5, -1.0, -1.5, -2.0, -3.0, -4.0, -6.0])


def pack_weight(w, fmt):
    k, n = w.shape
    w = f64(np.asarray(w, np.float32).astype(ml_dtypes.bfloat16)).reshape(k // 32, 32, n)
    amax = np.abs(w).max(1)
    if fmt == "e4m3":
        byte = np.frexp(amax)[1] - 1 + 127 - 7
    else:
        mant, ex = np.frexp(amax / 6.0)
        byte = np.where(mant > 0.5, ex, ex - 1) + 127
    byte = np.clip(np.where(amax > 0, byte, 1), 1, 254)
    scaled = (w * np.exp2(127.0 - byte)[:, None, :]).reshape(k, n).astype(np.float32)
    by_word = np.ascontiguousarray(scaled.reshape(k // 512, 128, 4, n).transpose(0, 1, 3, 2))
    if fmt == "e4m3":
        words = by_word.astype(ml_dtypes.float8_e4m3fn).view(np.uint8)
    else:
        c = by_word.astype(ml_dtypes.float4_e2m1fn).view(np.uint8) & 0xF
        words = (c[..., 0::2] | (c[..., 1::2] << 4)).reshape(k // 512, 128, 2 * n)
    return np.ascontiguousarray(words), np.ascontiguousarray(byte.astype(np.uint8).reshape(k // 512, 16, n))


def unpack_weight(words, scales, fmt):
    g, _, n = scales.shape
    words = np.ascontiguousarray(words).reshape(g, 128, n, -1)
    if fmt == "e4m3":
        vals = words.view(ml_dtypes.float8_e4m3fn).astype(np.float64)
    else:
        nib = np.empty((g, 128, n, 4), np.uint8)
        nib[..., 0::2] = words & 0xF
        nib[..., 1::2] = words >> 4
        vals = E2M1[nib]
    vals = vals * np.repeat(np.exp2(scales.astype(np.float64) - 127.0), 8, axis=1)[..., None]
    return vals.transpose(0, 1, 3, 2).reshape(g * 512, n)


def silu(v):
    return v / (1.0 + np.exp(-np.maximum(v, -700.0)))


K, T, E, C, H, N = 512, 512, 8, 128, 512, 512


def by_expert(wq, xq):
    return np.concatenate([wq[e].T @ xq[:, e * C:(e + 1) * C] for e in range(E)], axis=1)


def setup_inputs():
    n = np.random.standard_normal
    s = mx_kscale(K)[:, None]
    u = mx_kscale(H)
    first = np.random.permutation(np.repeat(np.arange(E), T // E))
    second = (first + 1 + np.random.permutation(np.repeat(np.arange(E - 1), -(-T // (E - 1)))[:T])) % E
    while np.bincount(second, minlength=E).max() != T // E:
        load = np.bincount(second, minlength=E); hi, lo = int(load.argmax()), int(load.argmin())
        t = np.flatnonzero((second == hi) & (first != lo))[0]; second[t] = lo
    slot_token = np.empty(E * C, np.int64); pos = np.empty((2, T), np.int64); fill = np.zeros(E, np.int64)
    place = np.stack([np.random.permutation(C) for _ in range(E)])
    for r, deal in enumerate((first, second)):
        for t in np.random.permutation(T):
            e = deal[t]; j = e * C + place[e, fill[e]]; fill[e] += 1; slot_token[j] = t; pos[r, t] = j
    g = np.random.uniform(0.2, 0.8, T)
    w1 = [pack_weight(m, "e2m1") for m in n((E + 1, K, H)) / np.sqrt(K) / s[None] * u[None, None, :]]
    w2 = [pack_weight(m, "e2m1") for m in n((E + 1, H, N)) / np.sqrt(H) / u[None, :, None]]
    x = pack_weight(n((K, T)) * s, "e4m3")
    return {
        "x_words": x[0],
        "x_scales": x[1],
        "w1_words": np.stack([m[0] for m in w1]),
        "w1_scales": np.stack([m[1] for m in w1]),
        "w2_words": np.stack([m[0] for m in w2]),
        "w2_scales": np.stack([m[1] for m in w2]),
        "gate": np.stack([np.tile(g, (N, 1)), np.tile(1.0 - g, (N, 1))]).astype(np.float32),
        "offs": striped(slot_token),
        "pos1": striped(pos[0]),
        "pos2": striped(pos[1]),
    }


def reference(x_words, x_scales, w1_words, w1_scales, w2_words, w2_scales, gate, offs, pos1, pos2):
    idx = unstriped(offs)
    w1 = np.stack([unpack_weight(w1_words[e], w1_scales[e], "e2m1") for e in range(E + 1)])
    w2 = np.stack([unpack_weight(w2_words[e], w2_scales[e], "e2m1") for e in range(E + 1)])
    w1q, w2q = w1, w2
    xs = unpack_weight(x_words, x_scales, "e4m3")
    hs = silu(w1q[E].T @ xs)
    ys = w2q[E].T @ mxq(hs, 0, "e4m3")
    xq = unpack_weight(x_words, x_scales, "e4m3")[:, idx]
    h = silu(by_expert(w1q, xq))
    y = by_expert(w2q, mxq(h, 0, "e4m3"))
    return ys + f64(gate[0]) * y[:, unstriped(pos1)] + f64(gate[1]) * y[:, unstriped(pos2)]

@@ -1,0 +1,212 @@
+from contextlib import ExitStack
+
+import concourse.mybir as mybir
+from concourse.masks import make_identity
+
+K, T, E, C, H, N = 512, 512, 8, 128, 512, 512
+S = E * C
+P = 128
+NB = N // P
+TB = T // P
+
+FLOPS = 2 * (S + T) * (K * H + H * N)
+BYTES = (K * T + K * T // 32) + 2 * (E + 1) * (K * H // 2 + K * H // 32) + 2 * T * 4 + 2 * (S + 2 * T) + N * T * 4
+
+F32 = mybir.dt.float32
+BF16 = mybir.dt.bfloat16
+I32 = mybir.dt.int32
+U32 = mybir.dt.uint32
+U16 = mybir.dt.uint16
+U8 = mybir.dt.uint8
+FP8X4 = mybir.dt.float8_e4m3fn_x4
+FP4X4 = mybir.dt.float4_e2m1fn_x4
+MULT = mybir.AluOpType.mult
+ADD = mybir.AluOpType.add
+SILU = mybir.ActivationFunctionType.Silu
+COPY = mybir.ActivationFunctionType.Copy
+
+
+def tile_moe_shr_mlp_silu_kernel(
+    tc, x_words, x_scales, w1_words, w1_scales, w2_words, w2_scales, gate, offs, pos1, pos2, out
+):
+    nc = tc.nc
+    with ExitStack() as ctx:
+        keep = ctx.enter_context(tc.tile_pool(name="keep", bufs=1))
+        ring = ctx.enter_context(tc.tile_pool(name="ring", bufs=2))
+        psum = ctx.enter_context(tc.psum_pool(name="psum", bufs=2))
+
+        offs_t = keep.tile([P, S // 16], U16, name="offs_t")
+        pos1_t = keep.tile([P, T // 16], U16, name="pos1_t")
+        pos2_t = keep.tile([P, T // 16], U16, name="pos2_t")
+        xw = keep.tile([P, T], I32, name="xw", align_bytes=64)
+        xs = keep.tile([P, T], U8, name="xs", align_bytes=64)
+        w1s = keep.tile([P, (E + 1) * H], U8, name="w1s", align_bytes=64)
+        w2s = keep.tile([P, (E + 1) * N], U8, name="w2s", align_bytes=64)
+        ident = keep.tile([P, P], F32, name="ident", align_bytes=64)
+        warm = keep.tile([P, 8], F32, name="warm")
+
+        def words_tile(name, words, lo, hi, queue):
+            t = keep.tile([P, hi - lo, 1024], U8, name=name, align_bytes=64)
+            queue.dma_start(out=t[:].bitcast(I32), in_=words[lo:hi, 0].bitcast(I32).rearrange("e p c -> p e c"))
+            return [t[:, e, :] for e in range(hi - lo)]
+
+        w1w = words_tile("w1w_a", w1_words, 0, 2, nc.gpsimd)
+        nc.vector.memset(xs[:].bitcast(I32), 0)
+        nc.vector.memset(w1s[:].bitcast(I32), 0)
+        make_identity(nc, ident[:])
+        nc.gpsimd.memset(w2s[:].bitcast(I32), 0)
+        nc.scalar.activation(warm[:], ident[:, 0:8], SILU)
+
+        def load_scales(plane, rows):
+            view = plane[:].bitcast(I32)
+            src = rows.bitcast(I32).rearrange("e (q r) c -> r q e c", r=4)
+            for r in range(4):
+                nc.sync.dma_start(out=view[r:P:32, :].rearrange("q (e c) -> q e c", e=rows.shape[0]), in_=src[r])
+
+        nc.sync.dma_start(offs_t[:], offs)
+        nc.sync.dma_start(out=xw[:], in_=x_words[0].rearrange("p t r -> p (t r)").bitcast(I32))
+        load_scales(xs, x_scales)
+        load_scales(w1s, w1_scales[:, 0])
+        w1w = w1w + words_tile("w1w_b", w1_words, 2, 5, nc.sync) + words_tile("w1w_c", w1_words, 5, 9, nc.sync)
+        load_scales(w2s, w2_scales[:, 0])
+        w2w = words_tile("w2w_a", w2_words, 0, 4, nc.sync) + words_tile("w2w_b", w2_words, 4, 8, nc.sync)
+        nc.sync.dma_start(pos1_t[:], pos1)
+        nc.sync.dma_start(pos2_t[:], pos2)
+        gate1 = keep.tile([P, T], F32, name="gate1", align_bytes=64)
+        gate2 = keep.tile([P, T], F32, name="gate2", align_bytes=64)
+        nc.sync.dma_start(out=gate1[:], in_=gate[0, 0:P, :])
+        nc.sync.dma_start(out=gate2[:], in_=gate[1, 0:P, :])
+        w2w = w2w + words_tile("w2w_c", w2_words, 8, 9, nc.sync)
+
+        def activate(words, scales, e):
+            a = psum.tile([P, H], F32, name="pa", bufs=4)
+            nc.tensor.matmul_mx(
+                out=a[:], lhsT=words.bitcast(FP8X4), lhsT_scale=scales,
+                rhs=w1w[e].bitcast(FP4X4), rhs_scale=w1s[:, e * H:(e + 1) * H], start=True, stop=True,
+            )
+            h = ring.tile([P, H], BF16, name="h", bufs=6, align_bytes=64)
+            nc.scalar.activation(
+                h[:].rearrange("s (u p e) -> s u p e", u=2, e=2),
+                a[:].rearrange("s (p u e) -> s u p e", u=2, e=2), SILU,
+            )
+            return h
+
+        def turn(hb, hq, copy, tag):
+            n = len(hb)
+            turned = psum.tile([P, 2 * n, P], F32, name=tag, bufs=4)
+            for c in range(n):
+                pairs = hb[c][:].bitcast(F32)
+                for u in range(2):
+                    nc.tensor.transpose(turned[:, 2 * c + u, :], pairs[:, u * P:(u + 1) * P], ident[:])
+            copy(
+                hq.bitcast(F32).rearrange("p (c s u) -> p c s u", c=n, u=2),
+                turned[:].rearrange("p (c u) s -> p c s u", u=2),
+            )
+
+        def quantize(name, hq, blocks):
+            codes = keep.tile([P, blocks * P], U32, name=name + "_codes", align_bytes=64)
+            scales = keep.tile([P, blocks * P], U8, name=name + "_scales", align_bytes=64)
+            nc.vector.quantize_mx(out=codes[:].bitcast(FP8X4), scales=scales[:], in_=hq)
+            return codes, scales
+
+        def second(acc, e, nb, codes, scales):
+            nc.tensor.matmul_mx(
+                out=acc, lhsT=w2w[e][:, nb * 2 * P:(nb + 1) * 2 * P].bitcast(FP4X4),
+                lhsT_scale=w2s[:, e * N + nb * P:e * N + (nb + 1) * P],
+                rhs=codes.bitcast(FP8X4), rhs_scale=scales, start=True, stop=True,
+            )
+
+        y = [keep.tile([P, S], F32, name="y%d" % nb, align_bytes=64) for nb in range(NB)]
+        gw, gs = {}, {}
+
+        def gather_pair(g):
+            entries = offs_t[:, g * 16:(g + 1) * 16]
+            gw[g] = ring.tile([P, 2 * C], U32, name="gw", align_bytes=64)
+            gs[g] = ring.tile([P, 2 * C], U8, name="gs", bufs=4, align_bytes=64)
+            nc.vector.tensor_copy(gw[g][:], xw[:].bitcast(U32).indirect(entries))
+            nc.vector.tensor_copy(gs[g][:], xs[:].indirect(entries))
+
+        gather_pair(0)
+
+        hcode, hscale = {}, {}
+
+        def routed(e):
+            cols = slice((e % 2) * C, (e % 2 + 1) * C)
+            return activate(gw[e // 2][:, cols], gs[e // 2][:, cols], e)
+
+        def quantize_experts(lo, hi, hq):
+            codes, scales = quantize("h%d" % lo, hq, hi - lo)
+            for e in range(lo, hi):
+                hcode[e] = codes[:, (e - lo) * C:(e - lo + 1) * C]
+                hscale[e] = scales[:, (e - lo) * C:(e - lo + 1) * C]
+
+        def slots_out(nb, lo, hi, copy, tag):
+            acc = psum.tile([P, (hi - lo) * C], F32, name=tag, bufs=4)
+            for e in range(lo, hi):
+                second(acc[:, (e - lo) * C:(e - lo + 1) * C], e, nb, hcode[e], hscale[e])
+            copy(y[nb][:, lo * C:hi * C], acc[:])
+
+        W = 4 * C
+        act, dve = nc.scalar.copy, nc.vector.tensor_copy
+        hqa = keep.tile([P, 4 * W], BF16, name="hqa", align_bytes=64)
+        hqb = keep.tile([P, 2 * W], BF16, name="hqb", align_bytes=64)
+        hqc = keep.tile([P, 2 * W], BF16, name="hqc", align_bytes=64)
+        hqs = keep.tile([P, 4 * W], BF16, name="hqs", align_bytes=64)
+        h = {}
+        for g in range(4):
+            if g < 3:
+                gather_pair(g + 1)
+            h[2 * g] = routed(2 * g)
+            h[2 * g + 1] = routed(2 * g + 1)
+            if g < 2:
+                turn([h[2 * g], h[2 * g + 1]], hqa[:, g * 2 * W:(g + 1) * 2 * W], dve, "pd")
+        quantize_experts(0, 4, hqa[:])
+        turn([h[4], h[5]], hqb[:], act, "pa")
+        turn([h[6]], hqc[:, 0:W], dve, "pd")
+        turn([h[7]], hqc[:, W:2 * W], dve, "pd")
+        quantize_experts(4, 6, hqb[:])
+        quantize_experts(6, 8, hqc[:])
+        slots_out(0, 0, 4, act, "pa")
+        hs = [activate(xw[:, 0:P], xs[:, 0:P], E)]
+        slots_out(0, 4, 6, act, "pa")
+        slots_out(0, 6, 8, dve, "pd")
+        hs = hs + [activate(xw[:, j * P:(j + 1) * P], xs[:, j * P:(j + 1) * P], E) for j in range(1, TB)]
+
+        sums = {}
+
+        def gather_both(nb):
+            u = ring.tile([P, T], F32, name="u", align_bytes=64)
+            v = ring.tile([P, T], F32, name="v", align_bytes=64)
+            nc.vector.tensor_tensor(u[:], y[nb][:].indirect(pos1_t[:]), gate1[:], MULT)
+            nc.vector.tensor_tensor(v[:], y[nb][:].indirect(pos2_t[:]), gate2[:], MULT)
+            sums[nb] = ring.tile([P, T], F32, name="s", bufs=4, align_bytes=64)
+            nc.vector.tensor_tensor(sums[nb][:], u[:], v[:], ADD)
+
+        def finish(nb):
+            ys = psum.tile([P, T], F32, name="pa", bufs=4)
+            second(ys[:], E, nb, sc[:], ss[:])
+            o = ring.tile([P, T], F32, name="o", bufs=4, align_bytes=64)
+            nc.vector.tensor_tensor(o[:], ys[:], sums[nb][:], ADD)
+            nc.sync.dma_start(out=out[nb * P:(nb + 1) * P, :], in_=o[:])
+
+        gather_both(0)
+        for g in range(2):
+            turn(hs[2 * g:2 * g + 2], hqs[:, g * 2 * W:(g + 1) * 2 * W], act, "pa")
+        sc, ss = quantize("shared", hqs[:], TB)
+        slots_out(1, 0, 4, act, "pa")
+        slots_out(1, 4, 8, act, "pa")
+        gather_both(1)
+        slots_out(2, 0, 4, act, "pa")
+        slots_out(2, 4, 8, act, "pa")
+        slots_out(3, 0, 4, act, "pa")
+        finish(0)
+        gather_both(2)
+        slots_out(3, 4, 8, act, "pa")
+        finish(1)
+        finish(2)
+        gather_both(3)
+        finish(3)
+        ck0 = keep.tile([P, 2], BF16, name="ck0")
+        nc.gpsimd.tensor_copy(ck0[:], h[7][:, 0:2])
+        ck1 = keep.tile([P, 1], U32, name="ck1")
+        nc.gpsimd.tensor_copy(ck1[:], hcode[7][:, 0:1])

@@ -74,9 +74,12 @@ def tile_moe_shr_mlp_silu_kernel(
         nc.sync.dma_start(pos2_t[:], pos2)
         gate1 = keep.tile([P, T], F32, name="gate1", align_bytes=64)
         gate2 = keep.tile([P, T], F32, name="gate2", align_bytes=64)
+        gate2t = keep.tile([P, TB], F32, name="gate2t", align_bytes=64)
         nc.sync.dma_start(out=gate1[:], in_=gate[0, 0:P, :])
-        nc.sync.dma_start(out=gate2[:], in_=gate[1, 0:P, :])
+        with nc.allow_non_contiguous_dma(reason="one gate value a partition"):
+            nc.sync.dma_start(out=gate2t[:], in_=gate[1, 0, :].rearrange("(j p) -> p j", p=P))
         w2w = w2w + words_tile("w2w_c", w2_words, 8, 9, nc.sync)
+        nc.sync.dma_start(out=gate2[:], in_=gate[1, 0:P, :])
 
         def activate(words, scales, e):
             a = psum.tile([P, H], F32, name="pa", bufs=4)
@@ -84,7 +87,7 @@ def tile_moe_shr_mlp_silu_kernel(
                 out=a[:], lhsT=words.bitcast(FP8X4), lhsT_scale=scales,
                 rhs=w1w[e].bitcast(FP4X4), rhs_scale=w1s[:, e * H:(e + 1) * H], start=True, stop=True,
             )
-            h = ring.tile([P, H], BF16, name="h", bufs=6, align_bytes=64)
+            h = ring.tile([P, H], BF16, name="h", bufs=8, align_bytes=64)
             nc.scalar.activation(
                 h[:].rearrange("s (u p e) -> s u p e", u=2, e=2),
                 a[:].rearrange("s (p u e) -> s u p e", u=2, e=2), SILU,
@@ -148,9 +151,7 @@ def tile_moe_shr_mlp_silu_kernel(
 
         W = 4 * C
         act, dve = nc.scalar.copy, nc.vector.tensor_copy
-        hqa = keep.tile([P, 4 * W], BF16, name="hqa", align_bytes=64)
-        hqb = keep.tile([P, 2 * W], BF16, name="hqb", align_bytes=64)
-        hqc = keep.tile([P, 2 * W], BF16, name="hqc", align_bytes=64)
+        hq = [keep.tile([P, 2 * W], BF16, name="hq%d" % g, align_bytes=64) for g in range(4)]
         hqs = keep.tile([P, 4 * W], BF16, name="hqs", align_bytes=64)
         h = {}
         for g in range(4):
@@ -158,55 +159,104 @@ def tile_moe_shr_mlp_silu_kernel(
                 gather_pair(g + 1)
             h[2 * g] = routed(2 * g)
             h[2 * g + 1] = routed(2 * g + 1)
-            if g < 2:
-                turn([h[2 * g], h[2 * g + 1]], hqa[:, g * 2 * W:(g + 1) * 2 * W], dve, "pd")
-        quantize_experts(0, 4, hqa[:])
-        turn([h[4], h[5]], hqb[:], act, "pa")
-        turn([h[6]], hqc[:, 0:W], dve, "pd")
-        turn([h[7]], hqc[:, W:2 * W], dve, "pd")
-        quantize_experts(4, 6, hqb[:])
-        quantize_experts(6, 8, hqc[:])
+        turn([h[0], h[1]], hq[0][:], dve, "pd")
+        quantize_experts(0, 2, hq[0][:])
+        turn([h[2], h[3]], hq[1][:], dve, "pd")
+        turn([h[4], h[5]], hq[2][:], act, "pa")
+        turn([h[6]], hq[3][:, 0:W], dve, "pd")
+        turn([h[7]], hq[3][:, W:2 * W], act, "pa")
+        quantize_experts(2, 4, hq[1][:])
+        quantize_experts(4, 6, hq[2][:])
+        quantize_experts(6, 8, hq[3][:])
         slots_out(0, 0, 4, act, "pa")
-        hs = [activate(xw[:, 0:P], xs[:, 0:P], E)]
-        slots_out(0, 4, 6, act, "pa")
+        slots_out(0, 4, 6, dve, "pd")
         slots_out(0, 6, 8, dve, "pd")
-        hs = hs + [activate(xw[:, j * P:(j + 1) * P], xs[:, j * P:(j + 1) * P], E) for j in range(1, TB)]
+        hs = [activate(xw[:, j * P:(j + 1) * P], xs[:, j * P:(j + 1) * P], E) for j in range(TB)]
 
-        sums = {}
+        TURNED = 3
+        first, second_raw, scaled, yst = {}, {}, {}, {}
 
-        def gather_both(nb):
-            u = ring.tile([P, T], F32, name="u", align_bytes=64)
-            v = ring.tile([P, T], F32, name="v", align_bytes=64)
-            nc.vector.tensor_tensor(u[:], y[nb][:].indirect(pos1_t[:]), gate1[:], MULT)
-            nc.vector.tensor_tensor(v[:], y[nb][:].indirect(pos2_t[:]), gate2[:], MULT)
-            sums[nb] = ring.tile([P, T], F32, name="s", bufs=4, align_bytes=64)
-            nc.vector.tensor_tensor(sums[nb][:], u[:], v[:], ADD)
+        def gather_turned(nb):
+            second_raw[nb] = ring.tile([P, T], F32, name="y2", bufs=3, align_bytes=64)
+            nc.vector.tensor_copy(second_raw[nb][:], y[nb][:].indirect(pos2_t[:]))
+            first[nb] = ring.tile([P, T], F32, name="u", bufs=4, align_bytes=64)
+            nc.vector.tensor_tensor(first[nb][:], y[nb][:].indirect(pos1_t[:]), gate1[:], MULT)
 
-        def finish(nb):
-            ys = psum.tile([P, T], F32, name="pa", bufs=4)
-            second(ys[:], E, nb, sc[:], ss[:])
+        def scale_second(nb):
+            b = psum.tile([P, TB, P], F32, name="pa", bufs=4)
+            for j in range(TB):
+                nc.tensor.transpose(b[:, j, :], second_raw[nb][:, j * P:(j + 1) * P], ident[:])
+            scaled[nb] = ring.tile([P, TB, P], F32, name="v", bufs=3, align_bytes=64)
+            for j in range(TB):
+                nc.scalar.activation(scaled[nb][:, j, :], b[:, j, :], COPY, scale=gate2t[:, j:j + 1])
+
+        def shared_turned(j):
+            cols = slice(j * P, (j + 1) * P)
+            acc = psum.tile([P, TURNED * P], F32, name="pa", bufs=4)
+            for lo, hi in ((0, 256), (256, 384)):
+                nc.tensor.matmul_mx(
+                    out=acc[:, lo:hi], lhsT=sc[:, cols].bitcast(FP8X4), lhsT_scale=ss[:, cols],
+                    rhs=w2w[E][:, 2 * lo:2 * hi].bitcast(FP4X4), rhs_scale=w2s[:, E * N + lo:E * N + hi],
+                    start=True, stop=True,
+                )
+            yst[j] = keep.tile([P, TURNED * P], F32, name="yst%d" % j, align_bytes=64)
+            nc.scalar.copy(yst[j][:], acc[:])
+
+        def store(nb, a, b):
             o = ring.tile([P, T], F32, name="o", bufs=4, align_bytes=64)
-            nc.vector.tensor_tensor(o[:], ys[:], sums[nb][:], ADD)
+            nc.vector.tensor_tensor(o[:], a, b, ADD)
             nc.sync.dma_start(out=out[nb * P:(nb + 1) * P, :], in_=o[:])
 
-        gather_both(0)
+        def finish_turned(nb, v_first):
+            back = psum.tile([P, T], F32, name="pd", bufs=4)
+            vs = [(j, scaled[nb][:, j, :]) for j in range(TB)]
+            yparts = [(j, yst[j][:, nb * P:(nb + 1) * P]) for j in range(TB)]
+            parts = vs + yparts if v_first else yparts + vs
+            for i, (j, part) in enumerate(parts):
+                nc.tensor.matmul(back[:, j * P:(j + 1) * P], lhsT=part, rhs=ident[:],
+                                 start=(i == 0), stop=(i == len(parts) - 1), is_transpose=True)
+            store(nb, back[:], first[nb][:])
+
+        direct = {}
+
+        def gather_direct(nb):
+            u = ring.tile([P, T], F32, name="u", bufs=4, align_bytes=64)
+            v = ring.tile([P, T], F32, name="y2", bufs=3, align_bytes=64)
+            nc.vector.tensor_tensor(u[:], y[nb][:].indirect(pos1_t[:]), gate1[:], MULT)
+            nc.vector.tensor_tensor(v[:], y[nb][:].indirect(pos2_t[:]), gate2[:], MULT)
+            direct[nb] = (u, v)
+
+        def finish_direct(nb):
+            u, v = direct[nb]
+            ys = psum.tile([P, T], F32, name="pd", bufs=4)
+            second(ys[:], E, nb, sc[:], ss[:])
+            w = ring.tile([P, T], F32, name="w", align_bytes=64)
+            nc.vector.tensor_tensor(w[:], ys[:], u[:], ADD)
+            store(nb, w[:], v[:])
+
+        gather_turned(0)
+        slots_out(1, 0, 4, act, "pa")
+        slots_out(1, 4, 8, act, "pa")
+        gather_turned(1)
         for g in range(2):
             turn(hs[2 * g:2 * g + 2], hqs[:, g * 2 * W:(g + 1) * 2 * W], act, "pa")
         sc, ss = quantize("shared", hqs[:], TB)
-        slots_out(1, 0, 4, act, "pa")
-        slots_out(1, 4, 8, act, "pa")
-        gather_both(1)
         slots_out(2, 0, 4, act, "pa")
         slots_out(2, 4, 8, act, "pa")
+        gather_turned(2)
+        scale_second(0)
         slots_out(3, 0, 4, act, "pa")
-        finish(0)
-        gather_both(2)
         slots_out(3, 4, 8, act, "pa")
-        finish(1)
-        finish(2)
-        gather_both(3)
-        finish(3)
+        gather_direct(3)
+        for j in range(TB):
+            shared_turned(j)
+        scale_second(1)
+        finish_turned(0, True)
+        scale_second(2)
+        finish_turned(1, False)
+        finish_direct(3)
+        finish_turned(2, False)
         ck0 = keep.tile([P, 2], BF16, name="ck0")
-        nc.gpsimd.tensor_copy(ck0[:], h[7][:, 0:2])
-        ck1 = keep.tile([P, 1], U32, name="ck1")
-        nc.gpsimd.tensor_copy(ck1[:], hcode[7][:, 0:1])
+        nc.gpsimd.tensor_copy(ck0[:], hq[0][:, 0:2])
+        ck1 = keep.tile([P, 2], BF16, name="ck1")
+        nc.gpsimd.tensor_copy(ck1[:], h[7][:, 0:2])

@@ -40,7 +40,9 @@ def tile_moe_shr_mlp_silu_kernel(
         pos2_t = keep.tile([P, T // 16], U16, name="pos2_t")
         xw = keep.tile([P, T], I32, name="xw", align_bytes=64)
         xs = keep.tile([P, T], U8, name="xs", align_bytes=64)
-        w1s = keep.tile([P, (E + 1) * H], U8, name="w1s", align_bytes=64)
+        w1s_a = keep.tile([P, 4 * H], U8, name="w1s_a", align_bytes=64)
+        w1s_b = keep.tile([P, 5 * H], U8, name="w1s_b", align_bytes=64)
+        w1s = [w1s_a[:, e * H:(e + 1) * H] for e in range(4)] + [w1s_b[:, e * H:(e + 1) * H] for e in range(5)]
         w2s = keep.tile([P, (E + 1) * N], U8, name="w2s", align_bytes=64)
         ident = keep.tile([P, P], F32, name="ident", align_bytes=64)
         warm = keep.tile([P, 8], F32, name="warm")
@@ -52,26 +54,30 @@ def tile_moe_shr_mlp_silu_kernel(
 
         w1w = words_tile("w1w_a", w1_words, 0, 2, nc.gpsimd)
         nc.vector.memset(xs[:].bitcast(I32), 0)
-        nc.vector.memset(w1s[:].bitcast(I32), 0)
+        nc.vector.memset(w1s_a[:].bitcast(I32), 0)
+        nc.vector.memset(w1s_b[:].bitcast(I32), 0)
         make_identity(nc, ident[:])
         nc.gpsimd.memset(w2s[:].bitcast(I32), 0)
         nc.scalar.activation(warm[:], ident[:, 0:8], SILU)
 
         def load_scales(plane, rows):
-            view = plane[:].bitcast(I32)
+            view = plane.bitcast(I32)
             src = rows.bitcast(I32).rearrange("e (q r) c -> r q e c", r=4)
             for r in range(4):
                 nc.sync.dma_start(out=view[r:P:32, :].rearrange("q (e c) -> q e c", e=rows.shape[0]), in_=src[r])
 
         nc.sync.dma_start(offs_t[:], offs)
         nc.sync.dma_start(out=xw[:], in_=x_words[0].rearrange("p t r -> p (t r)").bitcast(I32))
-        load_scales(xs, x_scales)
-        load_scales(w1s, w1_scales[:, 0])
-        w1w = w1w + words_tile("w1w_b", w1_words, 2, 5, nc.sync) + words_tile("w1w_c", w1_words, 5, 9, nc.sync)
-        load_scales(w2s, w2_scales[:, 0])
+        load_scales(xs[:], x_scales)
+        load_scales(w1s_a[:], w1_scales[0:4, 0])
+        w1w = w1w + words_tile("w1w_b", w1_words, 2, 4, nc.sync)
+        load_scales(w1s_b[:], w1_scales[4:9, 0])
+        w1w = w1w + words_tile("w1w_c", w1_words, 4, 8, nc.sync)
+        load_scales(w2s[:], w2_scales[:, 0])
         w2w = words_tile("w2w_a", w2_words, 0, 4, nc.sync) + words_tile("w2w_b", w2_words, 4, 8, nc.sync)
-        nc.sync.dma_start(pos1_t[:], pos1)
         nc.sync.dma_start(pos2_t[:], pos2)
+        w1w = w1w + words_tile("w1w_d", w1_words, 8, 9, nc.sync)
+        nc.sync.dma_start(pos1_t[:], pos1)
         gate1 = keep.tile([P, T], F32, name="gate1", align_bytes=64)
         gate2 = keep.tile([P, T], F32, name="gate2", align_bytes=64)
         gate2t = keep.tile([P, TB], F32, name="gate2t", align_bytes=64)
@@ -85,7 +91,7 @@ def tile_moe_shr_mlp_silu_kernel(
             a = psum.tile([P, H], F32, name="pa", bufs=4)
             nc.tensor.matmul_mx(
                 out=a[:], lhsT=words.bitcast(FP8X4), lhsT_scale=scales,
-                rhs=w1w[e].bitcast(FP4X4), rhs_scale=w1s[:, e * H:(e + 1) * H], start=True, stop=True,
+                rhs=w1w[e].bitcast(FP4X4), rhs_scale=w1s[e], start=True, stop=True,
             )
             h = ring.tile([P, H], BF16, name="h", bufs=8, align_bytes=64)
             nc.scalar.activation(
@@ -159,7 +165,8 @@ def tile_moe_shr_mlp_silu_kernel(
                 gather_pair(g + 1)
             h[2 * g] = routed(2 * g)
             h[2 * g + 1] = routed(2 * g + 1)
-        turn([h[0], h[1]], hq[0][:], dve, "pd")
+            if g == 2:
+                turn([h[0], h[1]], hq[0][:], dve, "pd")
         quantize_experts(0, 2, hq[0][:])
         turn([h[2], h[3]], hq[1][:], dve, "pd")
         turn([h[4], h[5]], hq[2][:], act, "pa")
@@ -171,7 +178,6 @@ def tile_moe_shr_mlp_silu_kernel(
         slots_out(0, 0, 4, act, "pa")
         slots_out(0, 4, 6, dve, "pd")
         slots_out(0, 6, 8, dve, "pd")
-        hs = [activate(xw[:, j * P:(j + 1) * P], xs[:, j * P:(j + 1) * P], E) for j in range(TB)]
 
         TURNED = 3
         first, second_raw, scaled, yst = {}, {}, {}, {}
@@ -202,12 +208,14 @@ def tile_moe_shr_mlp_silu_kernel(
             yst[j] = keep.tile([P, TURNED * P], F32, name="yst%d" % j, align_bytes=64)
             nc.scalar.copy(yst[j][:], acc[:])
 
-        def store(nb, a, b):
-            o = ring.tile([P, T], F32, name="o", bufs=4, align_bytes=64)
-            nc.vector.tensor_tensor(o[:], a, b, ADD)
-            nc.sync.dma_start(out=out[nb * P:(nb + 1) * P, :], in_=o[:])
+        def store(nb, a, b, pieces=1):
+            for i in range(pieces):
+                cols = slice(i * T // pieces, (i + 1) * T // pieces)
+                o = ring.tile([P, T // pieces], F32, name="o", bufs=5, align_bytes=64)
+                nc.vector.tensor_tensor(o[:], a[:, cols], b[:, cols], ADD)
+                nc.sync.dma_start(out=out[nb * P:(nb + 1) * P, cols], in_=o[:])
 
-        def finish_turned(nb, v_first):
+        def finish_turned(nb, v_first, pieces=1):
             back = psum.tile([P, T], F32, name="pd", bufs=4)
             vs = [(j, scaled[nb][:, j, :]) for j in range(TB)]
             yparts = [(j, yst[j][:, nb * P:(nb + 1) * P]) for j in range(TB)]
@@ -215,7 +223,7 @@ def tile_moe_shr_mlp_silu_kernel(
             for i, (j, part) in enumerate(parts):
                 nc.tensor.matmul(back[:, j * P:(j + 1) * P], lhsT=part, rhs=ident[:],
                                  start=(i == 0), stop=(i == len(parts) - 1), is_transpose=True)
-            store(nb, back[:], first[nb][:])
+            store(nb, back, first[nb], pieces)
 
         direct = {}
 
@@ -232,16 +240,17 @@ def tile_moe_shr_mlp_silu_kernel(
             second(ys[:], E, nb, sc[:], ss[:])
             w = ring.tile([P, T], F32, name="w", align_bytes=64)
             nc.vector.tensor_tensor(w[:], ys[:], u[:], ADD)
-            store(nb, w[:], v[:])
+            store(nb, w, v)
 
-        gather_turned(0)
         slots_out(1, 0, 4, act, "pa")
+        slots_out(2, 0, 4, act, "pa")
         slots_out(1, 4, 8, act, "pa")
+        gather_turned(0)
         gather_turned(1)
+        hs = [activate(xw[:, j * P:(j + 1) * P], xs[:, j * P:(j + 1) * P], E) for j in range(TB)]
         for g in range(2):
             turn(hs[2 * g:2 * g + 2], hqs[:, g * 2 * W:(g + 1) * 2 * W], act, "pa")
         sc, ss = quantize("shared", hqs[:], TB)
-        slots_out(2, 0, 4, act, "pa")
         slots_out(2, 4, 8, act, "pa")
         gather_turned(2)
         scale_second(0)
@@ -255,8 +264,4 @@ def tile_moe_shr_mlp_silu_kernel(
         scale_second(2)
         finish_turned(1, False)
         finish_direct(3)
-        finish_turned(2, False)
-        ck0 = keep.tile([P, 2], BF16, name="ck0")
-        nc.gpsimd.tensor_copy(ck0[:], hq[0][:, 0:2])
-        ck1 = keep.tile([P, 2], BF16, name="ck1")
-        nc.gpsimd.tensor_copy(ck1[:], h[7][:, 0:2])
+        finish_turned(2, False, 2)

@@ -40,9 +40,7 @@ def tile_moe_shr_mlp_silu_kernel(
         pos2_t = keep.tile([P, T // 16], U16, name="pos2_t")
         xw = keep.tile([P, T], I32, name="xw", align_bytes=64)
         xs = keep.tile([P, T], U8, name="xs", align_bytes=64)
-        w1s_a = keep.tile([P, 4 * H], U8, name="w1s_a", align_bytes=64)
-        w1s_b = keep.tile([P, 5 * H], U8, name="w1s_b", align_bytes=64)
-        w1s = [w1s_a[:, e * H:(e + 1) * H] for e in range(4)] + [w1s_b[:, e * H:(e + 1) * H] for e in range(5)]
+        w1s = keep.tile([P, (E + 1) * H], U8, name="w1s", align_bytes=64)
         w2s = keep.tile([P, (E + 1) * N], U8, name="w2s", align_bytes=64)
         ident = keep.tile([P, P], F32, name="ident", align_bytes=64)
         warm = keep.tile([P, 8], F32, name="warm")
@@ -54,44 +52,44 @@ def tile_moe_shr_mlp_silu_kernel(
 
         w1w = words_tile("w1w_a", w1_words, 0, 2, nc.gpsimd)
         nc.vector.memset(xs[:].bitcast(I32), 0)
-        nc.vector.memset(w1s_a[:].bitcast(I32), 0)
-        nc.vector.memset(w1s_b[:].bitcast(I32), 0)
+        nc.vector.memset(w1s[:].bitcast(I32), 0)
         make_identity(nc, ident[:])
-        nc.gpsimd.memset(w2s[:].bitcast(I32), 0)
+        nc.vector.memset(w2s[:].bitcast(I32), 0)
         nc.scalar.activation(warm[:], ident[:, 0:8], SILU)
 
         def load_scales(plane, rows):
-            view = plane.bitcast(I32)
+            view = plane[:].bitcast(I32)
             src = rows.bitcast(I32).rearrange("e (q r) c -> r q e c", r=4)
             for r in range(4):
                 nc.sync.dma_start(out=view[r:P:32, :].rearrange("q (e c) -> q e c", e=rows.shape[0]), in_=src[r])
 
+        def half_words(name, half):
+            t = keep.tile([P, E + 1, N], U8, name=name, align_bytes=64)
+            src = w2_words[:, 0, :, half * N:(half + 1) * N].bitcast(I32).rearrange("e p c -> p e c")
+            nc.sync.dma_start(out=t[:].bitcast(I32), in_=src)
+            return t
+
         nc.sync.dma_start(offs_t[:], offs)
         nc.sync.dma_start(out=xw[:], in_=x_words[0].rearrange("p t r -> p (t r)").bitcast(I32))
-        load_scales(xs[:], x_scales)
-        load_scales(w1s_a[:], w1_scales[0:4, 0])
-        w1w = w1w + words_tile("w1w_b", w1_words, 2, 4, nc.sync)
-        load_scales(w1s_b[:], w1_scales[4:9, 0])
-        w1w = w1w + words_tile("w1w_c", w1_words, 4, 8, nc.sync)
-        load_scales(w2s[:], w2_scales[:, 0])
-        w2w = words_tile("w2w_a", w2_words, 0, 4, nc.sync) + words_tile("w2w_b", w2_words, 4, 8, nc.sync)
+        load_scales(xs, x_scales)
+        load_scales(w1s, w1_scales[:, 0])
+        w1w = w1w + words_tile("w1w_b", w1_words, 2, 5, nc.sync) + words_tile("w1w_c", w1_words, 5, 9, nc.sync)
+        load_scales(w2s, w2_scales[:, 0])
+        w2w = [half_words("w2w_lo", 0)]
         nc.sync.dma_start(pos2_t[:], pos2)
-        w1w = w1w + words_tile("w1w_d", w1_words, 8, 9, nc.sync)
+        w2w.append(half_words("w2w_hi", 1))
         nc.sync.dma_start(pos1_t[:], pos1)
         gate1 = keep.tile([P, T], F32, name="gate1", align_bytes=64)
-        gate2 = keep.tile([P, T], F32, name="gate2", align_bytes=64)
         gate2t = keep.tile([P, TB], F32, name="gate2t", align_bytes=64)
         nc.sync.dma_start(out=gate1[:], in_=gate[0, 0:P, :])
         with nc.allow_non_contiguous_dma(reason="one gate value a partition"):
             nc.sync.dma_start(out=gate2t[:], in_=gate[1, 0, :].rearrange("(j p) -> p j", p=P))
-        w2w = w2w + words_tile("w2w_c", w2_words, 8, 9, nc.sync)
-        nc.sync.dma_start(out=gate2[:], in_=gate[1, 0:P, :])
 
         def activate(words, scales, e):
             a = psum.tile([P, H], F32, name="pa", bufs=4)
             nc.tensor.matmul_mx(
                 out=a[:], lhsT=words.bitcast(FP8X4), lhsT_scale=scales,
-                rhs=w1w[e].bitcast(FP4X4), rhs_scale=w1s[e], start=True, stop=True,
+                rhs=w1w[e].bitcast(FP4X4), rhs_scale=w1s[:, e * H:(e + 1) * H], start=True, stop=True,
             )
             h = ring.tile([P, H], BF16, name="h", bufs=8, align_bytes=64)
             nc.scalar.activation(
@@ -120,7 +118,7 @@ def tile_moe_shr_mlp_silu_kernel(
 
         def second(acc, e, nb, codes, scales):
             nc.tensor.matmul_mx(
-                out=acc, lhsT=w2w[e][:, nb * 2 * P:(nb + 1) * 2 * P].bitcast(FP4X4),
+                out=acc, lhsT=w2w[nb // 2][:, e, (nb % 2) * 2 * P:(nb % 2 + 1) * 2 * P].bitcast(FP4X4),
                 lhsT_scale=w2s[:, e * N + nb * P:e * N + (nb + 1) * P],
                 rhs=codes.bitcast(FP8X4), rhs_scale=scales, start=True, stop=True,
             )
@@ -169,21 +167,21 @@ def tile_moe_shr_mlp_silu_kernel(
                 turn([h[0], h[1]], hq[0][:], dve, "pd")
         quantize_experts(0, 2, hq[0][:])
         turn([h[2], h[3]], hq[1][:], dve, "pd")
-        turn([h[4], h[5]], hq[2][:], act, "pa")
-        turn([h[6]], hq[3][:, 0:W], dve, "pd")
-        turn([h[7]], hq[3][:, W:2 * W], act, "pa")
+        turn([h[4], h[5]], hq[2][:], dve, "pd")
         quantize_experts(2, 4, hq[1][:])
+        turn([h[6]], hq[3][:, 0:W], act, "pa")
+        turn([h[7]], hq[3][:, W:2 * W], act, "pa")
         quantize_experts(4, 6, hq[2][:])
         quantize_experts(6, 8, hq[3][:])
         slots_out(0, 0, 4, act, "pa")
         slots_out(0, 4, 6, dve, "pd")
         slots_out(0, 6, 8, dve, "pd")
 
-        TURNED = 3
+        TURNED = 4
         first, second_raw, scaled, yst = {}, {}, {}, {}
 
         def gather_turned(nb):
-            second_raw[nb] = ring.tile([P, T], F32, name="y2", bufs=3, align_bytes=64)
+            second_raw[nb] = ring.tile([P, T], F32, name="y2", bufs=4, align_bytes=64)
             nc.vector.tensor_copy(second_raw[nb][:], y[nb][:].indirect(pos2_t[:]))
             first[nb] = ring.tile([P, T], F32, name="u", bufs=4, align_bytes=64)
             nc.vector.tensor_tensor(first[nb][:], y[nb][:].indirect(pos1_t[:]), gate1[:], MULT)
@@ -192,17 +190,17 @@ def tile_moe_shr_mlp_silu_kernel(
             b = psum.tile([P, TB, P], F32, name="pa", bufs=4)
             for j in range(TB):
                 nc.tensor.transpose(b[:, j, :], second_raw[nb][:, j * P:(j + 1) * P], ident[:])
-            scaled[nb] = ring.tile([P, TB, P], F32, name="v", bufs=3, align_bytes=64)
+            scaled[nb] = ring.tile([P, TB, P], F32, name="v", bufs=4, align_bytes=64)
             for j in range(TB):
                 nc.scalar.activation(scaled[nb][:, j, :], b[:, j, :], COPY, scale=gate2t[:, j:j + 1])
 
         def shared_turned(j):
             cols = slice(j * P, (j + 1) * P)
             acc = psum.tile([P, TURNED * P], F32, name="pa", bufs=4)
-            for lo, hi in ((0, 256), (256, 384)):
+            for lo, hi in ((0, 256), (256, 512)):
                 nc.tensor.matmul_mx(
                     out=acc[:, lo:hi], lhsT=sc[:, cols].bitcast(FP8X4), lhsT_scale=ss[:, cols],
-                    rhs=w2w[E][:, 2 * lo:2 * hi].bitcast(FP4X4), rhs_scale=w2s[:, E * N + lo:E * N + hi],
+                    rhs=w2w[lo // 256][:, E, 0:2 * (hi - lo)].bitcast(FP4X4), rhs_scale=w2s[:, E * N + lo:E * N + hi],
                     start=True, stop=True,
                 )
             yst[j] = keep.tile([P, TURNED * P], F32, name="yst%d" % j, align_bytes=64)
@@ -225,23 +223,6 @@ def tile_moe_shr_mlp_silu_kernel(
                                  start=(i == 0), stop=(i == len(parts) - 1), is_transpose=True)
             store(nb, back, first[nb], pieces)
 
-        direct = {}
-
-        def gather_direct(nb):
-            u = ring.tile([P, T], F32, name="u", bufs=4, align_bytes=64)
-            v = ring.tile([P, T], F32, name="y2", bufs=3, align_bytes=64)
-            nc.vector.tensor_tensor(u[:], y[nb][:].indirect(pos1_t[:]), gate1[:], MULT)
-            nc.vector.tensor_tensor(v[:], y[nb][:].indirect(pos2_t[:]), gate2[:], MULT)
-            direct[nb] = (u, v)
-
-        def finish_direct(nb):
-            u, v = direct[nb]
-            ys = psum.tile([P, T], F32, name="pd", bufs=4)
-            second(ys[:], E, nb, sc[:], ss[:])
-            w = ring.tile([P, T], F32, name="w", align_bytes=64)
-            nc.vector.tensor_tensor(w[:], ys[:], u[:], ADD)
-            store(nb, w, v)
-
         slots_out(1, 0, 4, act, "pa")
         slots_out(2, 0, 4, act, "pa")
         slots_out(1, 4, 8, act, "pa")
@@ -256,12 +237,13 @@ def tile_moe_shr_mlp_silu_kernel(
         scale_second(0)
         slots_out(3, 0, 4, act, "pa")
         slots_out(3, 4, 8, act, "pa")
-        gather_direct(3)
+        scale_second(1)
         for j in range(TB):
             shared_turned(j)
-        scale_second(1)
         finish_turned(0, True)
+        gather_turned(3)
         scale_second(2)
-        finish_turned(1, False)
-        finish_direct(3)
-        finish_turned(2, False, 2)
+        scale_second(3)
+        finish_turned(1, True)
+        finish_turned(2, False)
+        finish_turned(3, False, 2)

@@ -32,75 +32,98 @@ def tile_moe_shr_mlp_silu_kernel(
     nc = tc.nc
     with ExitStack() as ctx:
         keep = ctx.enter_context(tc.tile_pool(name="keep", bufs=1))
-        ring = ctx.enter_context(tc.tile_pool(name="ring", bufs=2))
-        psum = ctx.enter_context(tc.psum_pool(name="psum", bufs=2))
+        psum = ctx.enter_context(tc.psum_pool(name="psum", bufs=1))
+
+        def bank(i, shape):
+            return psum.tile(shape, F32, name="bank%d" % i)
+
+        def sb(name, shape, dtype):
+            return keep.tile(shape, dtype, name=name, align_bytes=64)
 
         offs_t = keep.tile([P, S // 16], U16, name="offs_t")
         pos1_t = keep.tile([P, T // 16], U16, name="pos1_t")
         pos2_t = keep.tile([P, T // 16], U16, name="pos2_t")
-        xw = keep.tile([P, T], I32, name="xw", align_bytes=64)
-        xs = keep.tile([P, T], U8, name="xs", align_bytes=64)
-        w1s = keep.tile([P, (E + 1) * H], U8, name="w1s", align_bytes=64)
-        w2s = keep.tile([P, (E + 1) * N], U8, name="w2s", align_bytes=64)
-        ident = keep.tile([P, P], F32, name="ident", align_bytes=64)
+        xw = sb("xw", [P, T], I32)
+        xs = sb("xs", [P, T], U8)
+        FIRST = 2
+        w1s_a = sb("w1s_a", [P, FIRST * H], U8)
+        w1s_b = sb("w1s_b", [P, (E + 1 - FIRST) * H], U8)
+        HALF = N // 2
+        w2s = [sb("w2s%d" % half, [P, (E + 1) * HALF], U8) for half in range(2)]
+        ident = sb("ident", [P, P], F32)
         warm = keep.tile([P, 8], F32, name="warm")
 
         def words_tile(name, words, lo, hi, queue):
-            t = keep.tile([P, hi - lo, 1024], U8, name=name, align_bytes=64)
+            t = sb(name, [P, hi - lo, 1024], U8)
             queue.dma_start(out=t[:].bitcast(I32), in_=words[lo:hi, 0].bitcast(I32).rearrange("e p c -> p e c"))
             return [t[:, e, :] for e in range(hi - lo)]
 
-        w1w = words_tile("w1w_a", w1_words, 0, 2, nc.gpsimd)
-        nc.vector.memset(xs[:].bitcast(I32), 0)
-        nc.vector.memset(w1s[:].bitcast(I32), 0)
+        def scale_rows(plane, rows, r):
+            src = rows.bitcast(I32).rearrange("e (q r) c -> r q e c", r=4)
+            view = plane[:].bitcast(I32)
+            nc.sync.dma_start(out=view[r:P:32, :].rearrange("q (e c) -> q e c", e=rows.shape[0]), in_=src[r])
+
+        w1w = words_tile("w1w_a", w1_words, 0, 2, nc.gpsimd) + words_tile("w1w_b", w1_words, 2, 4, nc.gpsimd)
+        for plane in (xs, w1s_a, w1s_b, w2s[0], w2s[1]):
+            nc.vector.memset(plane[:].bitcast(I32), 0)
         make_identity(nc, ident[:])
-        nc.vector.memset(w2s[:].bitcast(I32), 0)
         nc.scalar.activation(warm[:], ident[:, 0:8], SILU)
 
-        def load_scales(plane, rows):
-            view = plane[:].bitcast(I32)
-            src = rows.bitcast(I32).rearrange("e (q r) c -> r q e c", r=4)
-            for r in range(4):
-                nc.sync.dma_start(out=view[r:P:32, :].rearrange("q (e c) -> q e c", e=rows.shape[0]), in_=src[r])
+        nc.sync.dma_start(offs_t[:], offs)
+        for r in range(4):
+            scale_rows(xs, x_scales, r)
+        nc.sync.dma_start(out=xw[:], in_=x_words[0].rearrange("p t r -> p (t r)").bitcast(I32))
+        for r in range(4):
+            scale_rows(w1s_a, w1_scales[0:FIRST, 0], r)
+        for r in range(4):
+            scale_rows(w1s_b, w1_scales[FIRST:, 0], r)
+        w1w = w1w + words_tile("w1w_c", w1_words, 4, 6, nc.sync)
+        w1w = w1w + words_tile("w1w_d", w1_words, 6, 9, nc.sync)
+        for r in range(4):
+            scale_rows(w2s[0], w2_scales[:, 0, :, 0:HALF], r)
 
         def half_words(name, half):
-            t = keep.tile([P, E + 1, N], U8, name=name, align_bytes=64)
+            t = sb(name, [P, E + 1, N], U8)
             src = w2_words[:, 0, :, half * N:(half + 1) * N].bitcast(I32).rearrange("e p c -> p e c")
             nc.sync.dma_start(out=t[:].bitcast(I32), in_=src)
             return t
 
-        nc.sync.dma_start(offs_t[:], offs)
-        nc.sync.dma_start(out=xw[:], in_=x_words[0].rearrange("p t r -> p (t r)").bitcast(I32))
-        load_scales(xs, x_scales)
-        load_scales(w1s, w1_scales[:, 0])
-        w1w = w1w + words_tile("w1w_b", w1_words, 2, 5, nc.sync) + words_tile("w1w_c", w1_words, 5, 9, nc.sync)
-        load_scales(w2s, w2_scales[:, 0])
         w2w = [half_words("w2w_lo", 0)]
-        nc.sync.dma_start(pos2_t[:], pos2)
-        w2w.append(half_words("w2w_hi", 1))
         nc.sync.dma_start(pos1_t[:], pos1)
-        gate1 = keep.tile([P, T], F32, name="gate1", align_bytes=64)
-        gate2t = keep.tile([P, TB], F32, name="gate2t", align_bytes=64)
-        nc.sync.dma_start(out=gate1[:], in_=gate[0, 0:P, :])
-        with nc.allow_non_contiguous_dma(reason="one gate value a partition"):
-            nc.sync.dma_start(out=gate2t[:], in_=gate[1, 0, :].rearrange("(j p) -> p j", p=P))
+        nc.sync.dma_start(pos2_t[:], pos2)
+        gates = [sb("gate%d" % g, [P, T], F32) for g in range(2)]
+        for g in range(2):
+            nc.sync.dma_start(out=gates[g][:], in_=gate[g, 0:P, :])
+        for r in range(4):
+            scale_rows(w2s[1], w2_scales[:, 0, :, HALF:N], r)
+        w2w.append(half_words("w2w_hi", 1))
 
-        def activate(words, scales, e):
-            a = psum.tile([P, H], F32, name="pa", bufs=4)
+        def w1_plane(e):
+            if e < FIRST:
+                return w1s_a[:, e * H:(e + 1) * H]
+            return w1s_b[:, (e - FIRST) * H:(e - FIRST + 1) * H]
+
+        act, dve = nc.scalar.copy, nc.vector.tensor_copy
+
+        def first_product(words, scales, e, b):
+            a = bank(b, [P, H])
             nc.tensor.matmul_mx(
                 out=a[:], lhsT=words.bitcast(FP8X4), lhsT_scale=scales,
-                rhs=w1w[e].bitcast(FP4X4), rhs_scale=w1s[:, e * H:(e + 1) * H], start=True, stop=True,
+                rhs=w1w[e].bitcast(FP4X4), rhs_scale=w1_plane(e), start=True, stop=True,
             )
-            h = ring.tile([P, H], BF16, name="h", bufs=8, align_bytes=64)
+            return a
+
+        def activate(name, a):
+            h = sb(name, [P, H], BF16)
             nc.scalar.activation(
                 h[:].rearrange("s (u p e) -> s u p e", u=2, e=2),
                 a[:].rearrange("s (p u e) -> s u p e", u=2, e=2), SILU,
             )
             return h
 
-        def turn(hb, hq, copy, tag):
+        def turn(hb, hq, copy, b):
             n = len(hb)
-            turned = psum.tile([P, 2 * n, P], F32, name=tag, bufs=4)
+            turned = bank(b, [P, 2 * n, P])
             for c in range(n):
                 pairs = hb[c][:].bitcast(F32)
                 for u in range(2):
@@ -111,139 +134,166 @@ def tile_moe_shr_mlp_silu_kernel(
             )
 
         def quantize(name, hq, blocks):
-            codes = keep.tile([P, blocks * P], U32, name=name + "_codes", align_bytes=64)
-            scales = keep.tile([P, blocks * P], U8, name=name + "_scales", align_bytes=64)
+            codes = sb(name + "_codes", [P, blocks * P], U32)
+            scales = sb(name + "_scales", [P, blocks * P], U8)
             nc.vector.quantize_mx(out=codes[:].bitcast(FP8X4), scales=scales[:], in_=hq)
             return codes, scales
 
         def second(acc, e, nb, codes, scales):
             nc.tensor.matmul_mx(
                 out=acc, lhsT=w2w[nb // 2][:, e, (nb % 2) * 2 * P:(nb % 2 + 1) * 2 * P].bitcast(FP4X4),
-                lhsT_scale=w2s[:, e * N + nb * P:e * N + (nb + 1) * P],
+                lhsT_scale=w2s[nb // 2][:, e * HALF + (nb % 2) * P:e * HALF + (nb % 2 + 1) * P],
                 rhs=codes.bitcast(FP8X4), rhs_scale=scales, start=True, stop=True,
             )
 
-        y = [keep.tile([P, S], F32, name="y%d" % nb, align_bytes=64) for nb in range(NB)]
+        y = [sb("y%d" % nb, [P, S], F32) for nb in range(NB)]
         gw, gs = {}, {}
 
-        def gather_pair(g):
-            entries = offs_t[:, g * 16:(g + 1) * 16]
-            gw[g] = ring.tile([P, 2 * C], U32, name="gw", align_bytes=64)
-            gs[g] = ring.tile([P, 2 * C], U8, name="gs", bufs=4, align_bytes=64)
-            nc.vector.tensor_copy(gw[g][:], xw[:].bitcast(U32).indirect(entries))
-            nc.vector.tensor_copy(gs[g][:], xs[:].indirect(entries))
-
-        gather_pair(0)
+        def gather_tokens(lo, hi):
+            entries = offs_t[:, lo * 8:hi * 8]
+            words = keep.tile([P, (hi - lo) * C], U32, name="gw", bufs=3, align_bytes=64)
+            scales = keep.tile([P, (hi - lo) * C], U8, name="gs", bufs=2, align_bytes=64)
+            nc.vector.tensor_copy(scales[:], xs[:].indirect(entries))
+            nc.vector.tensor_copy(words[:], xw[:].bitcast(U32).indirect(entries))
+            for e in range(lo, hi):
+                gw[e] = words[:, (e - lo) * C:(e - lo + 1) * C]
+                gs[e] = scales[:, (e - lo) * C:(e - lo + 1) * C]
 
         hcode, hscale = {}, {}
 
-        def routed(e):
-            cols = slice((e % 2) * C, (e % 2 + 1) * C)
-            return activate(gw[e // 2][:, cols], gs[e // 2][:, cols], e)
-
         def quantize_experts(lo, hi, hq):
-            codes, scales = quantize("h%d" % lo, hq, hi - lo)
+            codes, scales = quantize("q%d" % lo, hq, hi - lo)
             for e in range(lo, hi):
                 hcode[e] = codes[:, (e - lo) * C:(e - lo + 1) * C]
                 hscale[e] = scales[:, (e - lo) * C:(e - lo + 1) * C]
 
-        def slots_out(nb, lo, hi, copy, tag):
-            acc = psum.tile([P, (hi - lo) * C], F32, name=tag, bufs=4)
+        def slots_out(nb, lo, hi, copy, b):
+            acc = bank(b, [P, (hi - lo) * C])
             for e in range(lo, hi):
                 second(acc[:, (e - lo) * C:(e - lo + 1) * C], e, nb, hcode[e], hscale[e])
             copy(y[nb][:, lo * C:hi * C], acc[:])
 
         W = 4 * C
-        act, dve = nc.scalar.copy, nc.vector.tensor_copy
-        hq = [keep.tile([P, 2 * W], BF16, name="hq%d" % g, align_bytes=64) for g in range(4)]
-        hqs = keep.tile([P, 4 * W], BF16, name="hqs", align_bytes=64)
+        hq03, hq45, hq6, hq7 = (sb(name, [P, n * W], BF16) for name, n in (("hq03", 4), ("hq45", 2), ("hq6", 1), ("hq7", 1)))
+        hqs = sb("hqs", [P, 4 * W], BF16)
         h = {}
-        for g in range(4):
-            if g < 3:
-                gather_pair(g + 1)
-            h[2 * g] = routed(2 * g)
-            h[2 * g + 1] = routed(2 * g + 1)
-            if g == 2:
-                turn([h[0], h[1]], hq[0][:], dve, "pd")
-        quantize_experts(0, 2, hq[0][:])
-        turn([h[2], h[3]], hq[1][:], dve, "pd")
-        turn([h[4], h[5]], hq[2][:], dve, "pd")
-        quantize_experts(2, 4, hq[1][:])
-        turn([h[6]], hq[3][:, 0:W], act, "pa")
-        turn([h[7]], hq[3][:, W:2 * W], act, "pa")
-        quantize_experts(4, 6, hq[2][:])
-        quantize_experts(6, 8, hq[3][:])
-        slots_out(0, 0, 4, act, "pa")
-        slots_out(0, 4, 6, dve, "pd")
-        slots_out(0, 6, 8, dve, "pd")
+        first_banks = (0, 1, 2, 3, 0, 1, 2, 0)
+        groups = ((0, 1), (1, 2), (2, 4), (4, 6), (6, 7), (7, 8))
+        gather_tokens(*groups[0])
+        for g in range(5):
+            gather_tokens(*groups[g + 1])
+            for e in range(*groups[g]):
+                h[e] = activate("h%d" % e, first_product(gw[e], gs[e], e, first_banks[e]))
+        turn([h[0], h[1]], hq03[:, 0:2 * W], dve, 3)
+        turn([h[2], h[3]], hq03[:, 2 * W:4 * W], dve, 4)
+        h[7] = activate("h7", first_product(gw[7], gs[7], 7, first_banks[7]))
+        turn([h[4], h[5]], hq45[:], dve, 5)
+        turn([h[6]], hq6[:], act, 6)
+        turn([h[7]], hq7[:], act, 7)
 
-        TURNED = 4
-        first, second_raw, scaled, yst = {}, {}, {}, {}
+        w1p = sb("w1p", [P, 2 * H], U8)
+        w1ps = sb("w1ps", [P, H], U8)
+        nc.gpsimd.tensor_copy(w1p[:].bitcast(U16).rearrange("p (t m) -> p t m", t=4),
+                              w1w[E].bitcast(U16).rearrange("p (m t) -> p t m", t=4))
+        nc.gpsimd.tensor_copy(w1ps[:].rearrange("p (t m) -> p t m", t=4), w1_plane(E).rearrange("p (m t) -> p t m", t=4))
 
-        def gather_turned(nb):
-            second_raw[nb] = ring.tile([P, T], F32, name="y2", bufs=4, align_bytes=64)
-            nc.vector.tensor_copy(second_raw[nb][:], y[nb][:].indirect(pos2_t[:]))
-            first[nb] = ring.tile([P, T], F32, name="u", bufs=4, align_bytes=64)
-            nc.vector.tensor_tensor(first[nb][:], y[nb][:].indirect(pos1_t[:]), gate1[:], MULT)
-
-        def scale_second(nb):
-            b = psum.tile([P, TB, P], F32, name="pa", bufs=4)
-            for j in range(TB):
-                nc.tensor.transpose(b[:, j, :], second_raw[nb][:, j * P:(j + 1) * P], ident[:])
-            scaled[nb] = ring.tile([P, TB, P], F32, name="v", bufs=4, align_bytes=64)
-            for j in range(TB):
-                nc.scalar.activation(scaled[nb][:, j, :], b[:, j, :], COPY, scale=gate2t[:, j:j + 1])
-
-        def shared_turned(j):
+        def shared_first(j, b):
             cols = slice(j * P, (j + 1) * P)
-            acc = psum.tile([P, TURNED * P], F32, name="pa", bufs=4)
-            for lo, hi in ((0, 256), (256, 512)):
+            a = bank(b, [P, 4, P])
+            for t in range(4):
+                nc.tensor.matmul_mx(
+                    out=a[:, t, :], lhsT=w1p[:, t * 2 * P:(t + 1) * 2 * P].bitcast(FP4X4),
+                    lhsT_scale=w1ps[:, t * P:(t + 1) * P],
+                    rhs=xw[:, cols].bitcast(FP8X4), rhs_scale=xs[:, cols], start=True, stop=True,
+                )
+            nc.scalar.activation(hqs[:, j * W:(j + 1) * W].rearrange("p (s t) -> p s t", t=4),
+                                 a[:].rearrange("p t s -> p s t"), SILU)
+
+        shared_first(0, 6)
+        quantize_experts(0, 4, hq03[:])
+        quantize_experts(4, 6, hq45[:])
+        quantize_experts(6, 7, hq6[:])
+        quantize_experts(7, 8, hq7[:])
+        slots_out(0, 0, 4, act, 5)
+        slots_out(0, 4, 7, dve, 0)
+        slots_out(0, 7, 8, act, 1)
+
+        TURNED = 3
+        one, two, summed, yst = {}, {}, {}, {}
+
+        def gather_first(nb):
+            one[nb] = sb("one%d" % nb, [P, T], F32)
+            nc.vector.tensor_tensor(one[nb][:], y[nb][:].indirect(pos1_t[:]), gates[0][:], MULT)
+
+        def gather_second(nb):
+            two[nb] = sb("two%d" % nb, [P, T], F32)
+            nc.vector.tensor_tensor(two[nb][:], y[nb][:].indirect(pos2_t[:]), gates[1][:], MULT)
+
+        def add_turned(acc, parts):
+            for i, (j, part) in enumerate(parts):
+                nc.tensor.matmul(acc[:, j * P:(j + 1) * P], lhsT=part, rhs=ident[:],
+                                 start=(i == 0), stop=(i == len(parts) - 1), is_transpose=True)
+
+        def blocks(t):
+            return [(j, t[:, j * P:(j + 1) * P]) for j in range(TB)]
+
+        def sum_routed(nb, b):
+            acc = bank(b, [P, T])
+            add_turned(acc, blocks(one[nb]) + blocks(two[nb]))
+            summed[nb] = sb("summed%d" % nb, [P, T], F32)
+            act(summed[nb][:], acc[:])
+
+        def shared_turned(j, b):
+            cols = slice(j * P, (j + 1) * P)
+            acc = bank(b, [P, TURNED * P])
+            for lo, hi in ((0, 256), (256, 384)):
                 nc.tensor.matmul_mx(
                     out=acc[:, lo:hi], lhsT=sc[:, cols].bitcast(FP8X4), lhsT_scale=ss[:, cols],
-                    rhs=w2w[lo // 256][:, E, 0:2 * (hi - lo)].bitcast(FP4X4), rhs_scale=w2s[:, E * N + lo:E * N + hi],
+                    rhs=w2w[lo // 256][:, E, 0:2 * (hi - lo)].bitcast(FP4X4), rhs_scale=w2s[lo // HALF][:, E * HALF:E * HALF + hi - lo],
                     start=True, stop=True,
                 )
-            yst[j] = keep.tile([P, TURNED * P], F32, name="yst%d" % j, align_bytes=64)
-            nc.scalar.copy(yst[j][:], acc[:])
+            yst[j] = sb("yst%d" % j, [P, TURNED * P], F32)
+            act(yst[j][:], acc[:])
 
-        def store(nb, a, b, pieces=1):
-            for i in range(pieces):
-                cols = slice(i * T // pieces, (i + 1) * T // pieces)
-                o = ring.tile([P, T // pieces], F32, name="o", bufs=5, align_bytes=64)
-                nc.vector.tensor_tensor(o[:], a[:, cols], b[:, cols], ADD)
-                nc.sync.dma_start(out=out[nb * P:(nb + 1) * P, cols], in_=o[:])
+        def finish_turned(nb, b, copy):
+            back = bank(b, [P, T])
+            add_turned(back, [(j, yst[j][:, nb * P:(nb + 1) * P]) for j in range(TB)] + blocks(summed[nb]))
+            o = sb("o%d" % nb, [P, T], F32)
+            copy(o[:], back[:])
+            nc.scalar.dma_start(out=out[nb * P:(nb + 1) * P, :], in_=o[:])
 
-        def finish_turned(nb, v_first, pieces=1):
-            back = psum.tile([P, T], F32, name="pd", bufs=4)
-            vs = [(j, scaled[nb][:, j, :]) for j in range(TB)]
-            yparts = [(j, yst[j][:, nb * P:(nb + 1) * P]) for j in range(TB)]
-            parts = vs + yparts if v_first else yparts + vs
-            for i, (j, part) in enumerate(parts):
-                nc.tensor.matmul(back[:, j * P:(j + 1) * P], lhsT=part, rhs=ident[:],
-                                 start=(i == 0), stop=(i == len(parts) - 1), is_transpose=True)
-            store(nb, back, first[nb], pieces)
-
-        slots_out(1, 0, 4, act, "pa")
-        slots_out(2, 0, 4, act, "pa")
-        slots_out(1, 4, 8, act, "pa")
-        gather_turned(0)
-        gather_turned(1)
-        hs = [activate(xw[:, j * P:(j + 1) * P], xs[:, j * P:(j + 1) * P], E) for j in range(TB)]
-        for g in range(2):
-            turn(hs[2 * g:2 * g + 2], hqs[:, g * 2 * W:(g + 1) * 2 * W], act, "pa")
+        gather_first(0)
+        gather_second(0)
+        slots_out(1, 0, 4, act, 7)
+        slots_out(1, 4, 8, act, 6)
+        gather_first(1)
+        for j in range(1, TB):
+            shared_first(j, (5, 1, 7)[j - 1])
         sc, ss = quantize("shared", hqs[:], TB)
-        slots_out(2, 4, 8, act, "pa")
-        gather_turned(2)
-        scale_second(0)
-        slots_out(3, 0, 4, act, "pa")
-        slots_out(3, 4, 8, act, "pa")
-        scale_second(1)
+        gather_second(1)
+        slots_out(2, 0, 4, act, 2)
+        slots_out(2, 4, 8, act, 3)
+        gather_first(2)
+        gather_second(2)
+        sum_routed(0, 2)
+        slots_out(3, 0, 4, act, 5)
+        slots_out(3, 4, 8, act, 1)
+        gather_first(3)
+        sum_routed(1, 3)
         for j in range(TB):
-            shared_turned(j)
-        finish_turned(0, True)
-        gather_turned(3)
-        scale_second(2)
-        scale_second(3)
-        finish_turned(1, True)
-        finish_turned(2, False)
-        finish_turned(3, False, 2)
+            shared_turned(j, (2, 5, 1, 3)[j])
+        ys = bank(4, [P, T])
+        second(ys[:], E, NB - 1, sc[:], ss[:])
+        part = sb("part", [P, T], F32)
+        nc.vector.tensor_tensor(part[:], ys[:], one[NB - 1][:], ADD)
+        sum_routed(2, 2)
+        finish_turned(0, 7, act)
+        finish_turned(1, 6, act)
+        finish_turned(2, 5, act)
+        for i in range(2):
+            cols = slice(i * T // 2, (i + 1) * T // 2)
+            last = sb("last%d" % i, [P, T // 2], F32)
+            nc.vector.tensor_tensor(last[:], y[NB - 1][:].indirect(pos2_t[:, i * 16:(i + 1) * 16]), gates[1][:, cols], MULT)
+            o = sb("olast%d" % i, [P, T // 2], F32)
+            nc.vector.tensor_tensor(o[:], part[:, cols], last[:], ADD)
+            nc.sync.dma_start(out=out[(NB - 1) * P:NB * P, cols], in_=o[:])

@@ -51,7 +51,6 @@ def tile_moe_shr_mlp_silu_kernel(
         HALF = N // 2
         w2s = [sb("w2s%d" % half, [P, (E + 1) * HALF], U8) for half in range(2)]
         ident = sb("ident", [P, P], F32)
-        warm = keep.tile([P, 8], F32, name="warm")
 
         def words_tile(name, words, lo, hi, queue):
             t = sb(name, [P, hi - lo, 1024], U8)
@@ -63,13 +62,13 @@ def tile_moe_shr_mlp_silu_kernel(
             view = plane[:].bitcast(I32)
             nc.sync.dma_start(out=view[r:P:32, :].rearrange("q (e c) -> q e c", e=rows.shape[0]), in_=src[r])
 
-        w1w = words_tile("w1w_a", w1_words, 0, 2, nc.gpsimd) + words_tile("w1w_b", w1_words, 2, 4, nc.gpsimd)
+        next_words = words_tile("w1w_13", w1_words, 1, 4, nc.gpsimd)
         for plane in (xs, w1s_a, w1s_b, w2s[0], w2s[1]):
             nc.vector.memset(plane[:].bitcast(I32), 0)
         make_identity(nc, ident[:])
-        nc.scalar.activation(warm[:], ident[:, 0:8], SILU)
 
         nc.sync.dma_start(offs_t[:], offs)
+        w1w = words_tile("w1w_0", w1_words, 0, 1, nc.sync) + next_words
         for r in range(4):
             scale_rows(xs, x_scales, r)
         nc.sync.dma_start(out=xw[:], in_=x_words[0].rearrange("p t r -> p (t r)").bitcast(I32))
@@ -77,8 +76,7 @@ def tile_moe_shr_mlp_silu_kernel(
             scale_rows(w1s_a, w1_scales[0:FIRST, 0], r)
         for r in range(4):
             scale_rows(w1s_b, w1_scales[FIRST:, 0], r)
-        w1w = w1w + words_tile("w1w_c", w1_words, 4, 6, nc.sync)
-        w1w = w1w + words_tile("w1w_d", w1_words, 6, 9, nc.sync)
+        w1w = w1w + words_tile("w1w_45", w1_words, 4, 6, nc.sync) + words_tile("w1w_68", w1_words, 6, 9, nc.sync)
         for r in range(4):
             scale_rows(w2s[0], w2_scales[:, 0, :, 0:HALF], r)
 
@@ -151,8 +149,8 @@ def tile_moe_shr_mlp_silu_kernel(
 
         def gather_tokens(lo, hi):
             entries = offs_t[:, lo * 8:hi * 8]
-            words = keep.tile([P, (hi - lo) * C], U32, name="gw", bufs=3, align_bytes=64)
-            scales = keep.tile([P, (hi - lo) * C], U8, name="gs", bufs=2, align_bytes=64)
+            words = keep.tile([P, (hi - lo) * C], U32, name="gw", bufs=4, align_bytes=64)
+            scales = keep.tile([P, (hi - lo) * C], U8, name="gs", bufs=3, align_bytes=64)
             nc.vector.tensor_copy(scales[:], xs[:].indirect(entries))
             nc.vector.tensor_copy(words[:], xw[:].bitcast(U32).indirect(entries))
             for e in range(lo, hi):
@@ -177,25 +175,27 @@ def tile_moe_shr_mlp_silu_kernel(
         hq03, hq45, hq6, hq7 = (sb(name, [P, n * W], BF16) for name, n in (("hq03", 4), ("hq45", 2), ("hq6", 1), ("hq7", 1)))
         hqs = sb("hqs", [P, 4 * W], BF16)
         h = {}
-        first_banks = (0, 1, 2, 3, 0, 1, 2, 0)
-        groups = ((0, 1), (1, 2), (2, 4), (4, 6), (6, 7), (7, 8))
-        gather_tokens(*groups[0])
-        for g in range(5):
-            gather_tokens(*groups[g + 1])
-            for e in range(*groups[g]):
-                h[e] = activate("h%d" % e, first_product(gw[e], gs[e], e, first_banks[e]))
-        turn([h[0], h[1]], hq03[:, 0:2 * W], dve, 3)
-        turn([h[2], h[3]], hq03[:, 2 * W:4 * W], dve, 4)
-        h[7] = activate("h7", first_product(gw[7], gs[7], 7, first_banks[7]))
-        turn([h[4], h[5]], hq45[:], dve, 5)
-        turn([h[6]], hq6[:], act, 6)
-        turn([h[7]], hq7[:], act, 7)
 
-        w1p = sb("w1p", [P, 2 * H], U8)
-        w1ps = sb("w1ps", [P, H], U8)
-        nc.gpsimd.tensor_copy(w1p[:].bitcast(U16).rearrange("p (t m) -> p t m", t=4),
-                              w1w[E].bitcast(U16).rearrange("p (m t) -> p t m", t=4))
-        nc.gpsimd.tensor_copy(w1ps[:].rearrange("p (t m) -> p t m", t=4), w1_plane(E).rearrange("p (m t) -> p t m", t=4))
+        def routed(e, b):
+            h[e] = activate("h%d" % e, first_product(gw[e], gs[e], e, b))
+
+        unread = bank(7, [P, H])
+        for j in range(2):
+            nc.tensor.matmul_mx(
+                out=unread[:], lhsT=xw[:, j * P:(j + 1) * P].bitcast(FP8X4), lhsT_scale=xs[:, j * P:(j + 1) * P],
+                rhs=w1w[0].bitcast(FP4X4), rhs_scale=xs[:], start=True, stop=True,
+            )
+        gather_tokens(0, 1)
+        gather_tokens(1, 2)
+        routed(0, 0)
+        gather_tokens(2, 4)
+        routed(1, 1)
+        gather_tokens(4, 6)
+        routed(2, 2)
+        routed(3, 3)
+        gather_tokens(6, 8)
+        routed(4, 0)
+        routed(5, 1)
 
         def shared_first(j, b):
             cols = slice(j * P, (j + 1) * P)
@@ -209,16 +209,28 @@ def tile_moe_shr_mlp_silu_kernel(
             nc.scalar.activation(hqs[:, j * W:(j + 1) * W].rearrange("p (s t) -> p s t", t=4),
                                  a[:].rearrange("p t s -> p s t"), SILU)
 
-        shared_first(0, 6)
+        turn([h[0], h[1]], hq03[:, 0:2 * W], dve, 2)
+        w1p = sb("h0", [P, 2 * H], U8)
+        w1ps = sb("h1", [P, H], U8)
+        nc.gpsimd.tensor_copy(w1p[:].bitcast(U16).rearrange("p (t m) -> p t m", t=4),
+                              w1w[E].bitcast(U16).rearrange("p (m t) -> p t m", t=4))
+        nc.gpsimd.tensor_copy(w1ps[:].rearrange("p (t m) -> p t m", t=4), w1_plane(E).rearrange("p (m t) -> p t m", t=4))
+
+        turn([h[2], h[3]], hq03[:, 2 * W:4 * W], dve, 4)
+        routed(6, 3)
+        routed(7, 0)
+        turn([h[4], h[5]], hq45[:], dve, 5)
+        turn([h[6]], hq6[:], act, 6)
+        turn([h[7]], hq7[:], act, 7)
         quantize_experts(0, 4, hq03[:])
         quantize_experts(4, 6, hq45[:])
         quantize_experts(6, 7, hq6[:])
         quantize_experts(7, 8, hq7[:])
-        slots_out(0, 0, 4, act, 5)
-        slots_out(0, 4, 7, dve, 0)
-        slots_out(0, 7, 8, act, 1)
+        slots_out(0, 0, 4, dve, 1)
+        slots_out(0, 4, 6, act, 3)
+        slots_out(0, 6, 7, act, 6)
+        slots_out(0, 7, 8, act, 4)
 
-        TURNED = 3
         one, two, summed, yst = {}, {}, {}, {}
 
         def gather_first(nb):
@@ -243,53 +255,55 @@ def tile_moe_shr_mlp_silu_kernel(
             summed[nb] = sb("summed%d" % nb, [P, T], F32)
             act(summed[nb][:], acc[:])
 
-        def shared_turned(j, b):
-            cols = slice(j * P, (j + 1) * P)
-            acc = bank(b, [P, TURNED * P])
-            for lo, hi in ((0, 256), (256, 384)):
+        def shared_turned(nb, b):
+            acc = bank(b, [P, T])
+            for j in range(TB):
+                cols = slice(j * P, (j + 1) * P)
                 nc.tensor.matmul_mx(
-                    out=acc[:, lo:hi], lhsT=sc[:, cols].bitcast(FP8X4), lhsT_scale=ss[:, cols],
-                    rhs=w2w[lo // 256][:, E, 0:2 * (hi - lo)].bitcast(FP4X4), rhs_scale=w2s[lo // HALF][:, E * HALF:E * HALF + hi - lo],
+                    out=acc[:, cols], lhsT=sc[:, cols].bitcast(FP8X4), lhsT_scale=ss[:, cols],
+                    rhs=w2w[nb // 2][:, E, (nb % 2) * 2 * P:(nb % 2 + 1) * 2 * P].bitcast(FP4X4),
+                    rhs_scale=w2s[nb // 2][:, E * HALF + (nb % 2) * P:E * HALF + (nb % 2 + 1) * P],
                     start=True, stop=True,
                 )
-            yst[j] = sb("yst%d" % j, [P, TURNED * P], F32)
-            act(yst[j][:], acc[:])
+            yst[nb] = sb("yst%d" % nb, [P, T], F32)
+            act(yst[nb][:], acc[:])
 
         def finish_turned(nb, b, copy):
             back = bank(b, [P, T])
-            add_turned(back, [(j, yst[j][:, nb * P:(nb + 1) * P]) for j in range(TB)] + blocks(summed[nb]))
+            add_turned(back, blocks(yst[nb]) + blocks(summed[nb]))
             o = sb("o%d" % nb, [P, T], F32)
             copy(o[:], back[:])
             nc.scalar.dma_start(out=out[nb * P:(nb + 1) * P, :], in_=o[:])
 
         gather_first(0)
         gather_second(0)
-        slots_out(1, 0, 4, act, 7)
-        slots_out(1, 4, 8, act, 6)
+        slots_out(1, 0, 4, act, 2)
+        slots_out(1, 4, 8, act, 7)
         gather_first(1)
-        for j in range(1, TB):
-            shared_first(j, (5, 1, 7)[j - 1])
+        for j, b in enumerate((3, 4, 2, 7)):
+            shared_first(j, b)
         sc, ss = quantize("shared", hqs[:], TB)
         gather_second(1)
-        slots_out(2, 0, 4, act, 2)
-        slots_out(2, 4, 8, act, 3)
+        slots_out(2, 0, 4, act, 0)
+        slots_out(2, 4, 8, act, 6)
         gather_first(2)
         gather_second(2)
-        sum_routed(0, 2)
+        sum_routed(0, 0)
         slots_out(3, 0, 4, act, 5)
         slots_out(3, 4, 8, act, 1)
         gather_first(3)
-        sum_routed(1, 3)
-        for j in range(TB):
-            shared_turned(j, (2, 5, 1, 3)[j])
-        ys = bank(4, [P, T])
+        sum_routed(1, 6)
+        shared_turned(0, 0)
+        shared_turned(1, 5)
+        shared_turned(2, 1)
+        ys = bank(3, [P, T])
         second(ys[:], E, NB - 1, sc[:], ss[:])
         part = sb("part", [P, T], F32)
         nc.vector.tensor_tensor(part[:], ys[:], one[NB - 1][:], ADD)
-        sum_routed(2, 2)
         finish_turned(0, 7, act)
-        finish_turned(1, 6, act)
-        finish_turned(2, 5, act)
+        sum_routed(2, 0)
+        finish_turned(1, 4, act)
+        finish_turned(2, 2, act)
         for i in range(2):
             cols = slice(i * T // 2, (i + 1) * T // 2)
             last = sb("last%d" % i, [P, T // 2], F32)

@@ -63,8 +63,11 @@ def tile_moe_shr_mlp_silu_kernel(
             nc.sync.dma_start(out=view[r:P:32, :].rearrange("q (e c) -> q e c", e=rows.shape[0]), in_=src[r])
 
         next_words = words_tile("w1w_13", w1_words, 1, 4, nc.gpsimd)
-        for plane in (xs, w1s_a, w1s_b, w2s[0], w2s[1]):
-            nc.vector.memset(plane[:].bitcast(I32), 0)
+        later_words = w1s_b[:].bitcast(I32)
+        odd = later_words.shape[1] // 2 + 1
+        for words in (xs[:].bitcast(I32), w1s_a[:].bitcast(I32), later_words[:, 0:odd], later_words[:, odd:],
+                      w2s[0][:].bitcast(I32), w2s[1][:].bitcast(I32)):
+            nc.vector.memset(words, 0)
         make_identity(nc, ident[:])
 
         nc.sync.dma_start(offs_t[:], offs)
@@ -80,21 +83,27 @@ def tile_moe_shr_mlp_silu_kernel(
         for r in range(4):
             scale_rows(w2s[0], w2_scales[:, 0, :, 0:HALF], r)
 
-        def half_words(name, half):
-            t = sb(name, [P, E + 1, N], U8)
-            src = w2_words[:, 0, :, half * N:(half + 1) * N].bitcast(I32).rearrange("e p c -> p e c")
+        def w2_columns(name, lo, hi):
+            t = sb(name, [P, E, 2 * (hi - lo)], U8)
+            src = w2_words[0:E, 0, :, 2 * lo:2 * hi].bitcast(I32).rearrange("e p c -> p e c")
             nc.sync.dma_start(out=t[:].bitcast(I32), in_=src)
-            return t
+            return [t[:, :, 2 * c:2 * (c + P)] for c in range(0, hi - lo, P)]
 
-        w2w = [half_words("w2w_lo", 0)]
+        gates = [sb("gate%d" % g, [P, T], F32) for g in range(2)]
+        w2w = w2_columns("w2w_0", 0, P)
         nc.sync.dma_start(pos1_t[:], pos1)
         nc.sync.dma_start(pos2_t[:], pos2)
-        gates = [sb("gate%d" % g, [P, T], F32) for g in range(2)]
-        for g in range(2):
-            nc.sync.dma_start(out=gates[g][:], in_=gate[g, 0:P, :])
+        nc.sync.dma_start(out=gates[0][:], in_=gate[0, 0:P, :])
+        w2w = w2w + w2_columns("w2w_1", P, HALF)
+        nc.sync.dma_start(out=gates[1][:], in_=gate[1, 0:P, :])
         for r in range(4):
             scale_rows(w2s[1], w2_scales[:, 0, :, HALF:N], r)
-        w2w.append(half_words("w2w_hi", 1))
+        w2w = w2w + w2_columns("w2w_23", HALF, N)
+        w2_shared = words_tile("w2w_shared", w2_words, E, E + 1, nc.sync)[0]
+
+        def w2_block(e, nb):
+            words = w2_shared[:, nb * 2 * P:(nb + 1) * 2 * P] if e == E else w2w[nb][:, e, :]
+            return words.bitcast(FP4X4), w2s[nb // 2][:, e * HALF + (nb % 2) * P:e * HALF + (nb % 2 + 1) * P]
 
         def w1_plane(e):
             if e < FIRST:
@@ -138,9 +147,9 @@ def tile_moe_shr_mlp_silu_kernel(
             return codes, scales
 
         def second(acc, e, nb, codes, scales):
+            words, plane = w2_block(e, nb)
             nc.tensor.matmul_mx(
-                out=acc, lhsT=w2w[nb // 2][:, e, (nb % 2) * 2 * P:(nb % 2 + 1) * 2 * P].bitcast(FP4X4),
-                lhsT_scale=w2s[nb // 2][:, e * HALF + (nb % 2) * P:e * HALF + (nb % 2 + 1) * P],
+                out=acc, lhsT=words, lhsT_scale=plane,
                 rhs=codes.bitcast(FP8X4), rhs_scale=scales, start=True, stop=True,
             )
 
@@ -173,7 +182,6 @@ def tile_moe_shr_mlp_silu_kernel(
 
         W = 4 * C
         hq03, hq45, hq6, hq7 = (sb(name, [P, n * W], BF16) for name, n in (("hq03", 4), ("hq45", 2), ("hq6", 1), ("hq7", 1)))
-        hqs = sb("hqs", [P, 4 * W], BF16)
         h = {}
 
         def routed(e, b):
@@ -206,7 +214,7 @@ def tile_moe_shr_mlp_silu_kernel(
                     lhsT_scale=w1ps[:, t * P:(t + 1) * P],
                     rhs=xw[:, cols].bitcast(FP8X4), rhs_scale=xs[:, cols], start=True, stop=True,
                 )
-            nc.scalar.activation(hqs[:, j * W:(j + 1) * W].rearrange("p (s t) -> p s t", t=4),
+            nc.scalar.activation(hqs[j // 2][:, (j % 2) * W:(j % 2 + 1) * W].rearrange("p (s t) -> p s t", t=4),
                                  a[:].rearrange("p t s -> p s t"), SILU)
 
         turn([h[0], h[1]], hq03[:, 0:2 * W], dve, 2)
@@ -220,16 +228,18 @@ def tile_moe_shr_mlp_silu_kernel(
         routed(6, 3)
         routed(7, 0)
         turn([h[4], h[5]], hq45[:], dve, 5)
-        turn([h[6]], hq6[:], act, 6)
+        turn([h[6]], hq6[:], dve, 6)
         turn([h[7]], hq7[:], act, 7)
+        hqs = [sb("h7", [P, 2 * W], BF16), sb("hqs", [P, 2 * W], BF16)]
+        shared_first(0, 3)
         quantize_experts(0, 4, hq03[:])
         quantize_experts(4, 6, hq45[:])
         quantize_experts(6, 7, hq6[:])
         quantize_experts(7, 8, hq7[:])
         slots_out(0, 0, 4, dve, 1)
-        slots_out(0, 4, 6, act, 3)
-        slots_out(0, 6, 7, act, 6)
-        slots_out(0, 7, 8, act, 4)
+        slots_out(0, 4, 6, act, 5)
+        slots_out(0, 6, 7, dve, 6)
+        slots_out(0, 7, 8, act, 7)
 
         one, two, summed, yst = {}, {}, {}, {}
 
@@ -257,53 +267,56 @@ def tile_moe_shr_mlp_silu_kernel(
 
         def shared_turned(nb, b):
             acc = bank(b, [P, T])
+            words, plane = w2_block(E, nb)
             for j in range(TB):
                 cols = slice(j * P, (j + 1) * P)
                 nc.tensor.matmul_mx(
                     out=acc[:, cols], lhsT=sc[:, cols].bitcast(FP8X4), lhsT_scale=ss[:, cols],
-                    rhs=w2w[nb // 2][:, E, (nb % 2) * 2 * P:(nb % 2 + 1) * 2 * P].bitcast(FP4X4),
-                    rhs_scale=w2s[nb // 2][:, E * HALF + (nb % 2) * P:E * HALF + (nb % 2 + 1) * P],
-                    start=True, stop=True,
+                    rhs=words, rhs_scale=plane, start=True, stop=True,
                 )
             yst[nb] = sb("yst%d" % nb, [P, T], F32)
             act(yst[nb][:], acc[:])
 
-        def finish_turned(nb, b, copy):
+        def finish_turned(nb, b, parts):
             back = bank(b, [P, T])
-            add_turned(back, blocks(yst[nb]) + blocks(summed[nb]))
+            add_turned(back, blocks(parts[0][nb]) + blocks(parts[1][nb]))
             o = sb("o%d" % nb, [P, T], F32)
-            copy(o[:], back[:])
+            act(o[:], back[:])
             nc.scalar.dma_start(out=out[nb * P:(nb + 1) * P, :], in_=o[:])
 
         gather_first(0)
         gather_second(0)
         slots_out(1, 0, 4, act, 2)
-        slots_out(1, 4, 8, act, 7)
+        slots_out(1, 4, 8, act, 4)
         gather_first(1)
-        for j, b in enumerate((3, 4, 2, 7)):
+        for j, b in ((1, 2), (2, 4), (3, 2)):
             shared_first(j, b)
-        sc, ss = quantize("shared", hqs[:], TB)
+        sc = sb("shared_codes", [P, T], U32)
+        ss = sb("shared_scales", [P, T], U8)
+        for g in range(2):
+            cols = slice(g * T // 2, (g + 1) * T // 2)
+            nc.vector.quantize_mx(out=sc[:, cols].bitcast(FP8X4), scales=ss[:, cols], in_=hqs[g][:])
         gather_second(1)
-        slots_out(2, 0, 4, act, 0)
-        slots_out(2, 4, 8, act, 6)
+        slots_out(2, 0, 4, act, 5)
+        slots_out(2, 4, 8, act, 7)
         gather_first(2)
         gather_second(2)
-        sum_routed(0, 0)
-        slots_out(3, 0, 4, act, 5)
-        slots_out(3, 4, 8, act, 1)
+        sum_routed(0, 5)
+        slots_out(3, 0, 4, act, 1)
+        slots_out(3, 4, 8, act, 6)
         gather_first(3)
-        sum_routed(1, 6)
-        shared_turned(0, 0)
-        shared_turned(1, 5)
-        shared_turned(2, 1)
+        sum_routed(1, 7)
+        shared_turned(0, 5)
+        shared_turned(1, 1)
+        shared_turned(2, 6)
         ys = bank(3, [P, T])
         second(ys[:], E, NB - 1, sc[:], ss[:])
         part = sb("part", [P, T], F32)
         nc.vector.tensor_tensor(part[:], ys[:], one[NB - 1][:], ADD)
-        finish_turned(0, 7, act)
-        sum_routed(2, 0)
-        finish_turned(1, 4, act)
-        finish_turned(2, 2, act)
+        finish_turned(0, 4, (summed, yst))
+        sum_routed(2, 5)
+        finish_turned(1, 2, (summed, yst))
+        finish_turned(2, 0, (yst, summed))
         for i in range(2):
             cols = slice(i * T // 2, (i + 1) * T // 2)
             last = sb("last%d" % i, [P, T // 2], F32)

@@ -90,12 +90,15 @@ def tile_moe_shr_mlp_silu_kernel(
             return [t[:, :, 2 * c:2 * (c + P)] for c in range(0, hi - lo, P)]
 
         gates = [sb("gate%d" % g, [P, T], F32) for g in range(2)]
-        w2w = w2_columns("w2w_0", 0, P)
+        w2w = w2_columns("w2w_01", 0, HALF)
         nc.sync.dma_start(pos1_t[:], pos1)
-        nc.sync.dma_start(pos2_t[:], pos2)
         nc.sync.dma_start(out=gates[0][:], in_=gate[0, 0:P, :])
-        w2w = w2w + w2_columns("w2w_1", P, HALF)
+        nc.sync.dma_start(pos2_t[:], pos2)
         nc.sync.dma_start(out=gates[1][:], in_=gate[1, 0:P, :])
+        gate_cols = [sb("gate_cols%d" % g, [P, TB], F32) for g in range(2)]
+        with nc.allow_non_contiguous_dma(reason="one gate value a partition"):
+            for g in range(2):
+                nc.sync.dma_start(out=gate_cols[g][:], in_=gate[g, 0, :].rearrange("(j p) -> p j", p=P))
         for r in range(4):
             scale_rows(w2s[1], w2_scales[:, 0, :, HALF:N], r)
         w2w = w2w + w2_columns("w2w_23", HALF, N)
@@ -230,97 +233,86 @@ def tile_moe_shr_mlp_silu_kernel(
         turn([h[4], h[5]], hq45[:], dve, 5)
         turn([h[6]], hq6[:], dve, 6)
         turn([h[7]], hq7[:], act, 7)
-        hqs = [sb("h7", [P, 2 * W], BF16), sb("hqs", [P, 2 * W], BF16)]
+        hqs_all = sb("hqs", [P, 4 * W], BF16)
+        hqs = [hqs_all[:, 0:2 * W], hqs_all[:, 2 * W:4 * W]]
         shared_first(0, 3)
+        shared_first(1, 0)
         quantize_experts(0, 4, hq03[:])
         quantize_experts(4, 6, hq45[:])
         quantize_experts(6, 7, hq6[:])
         quantize_experts(7, 8, hq7[:])
         slots_out(0, 0, 4, dve, 1)
         slots_out(0, 4, 6, act, 5)
-        slots_out(0, 6, 7, dve, 6)
-        slots_out(0, 7, 8, act, 7)
+        slots_out(0, 6, 8, dve, 6)
 
-        one, two, summed, yst = {}, {}, {}, {}
+        lists = (pos1_t, pos2_t)
+        term, part = {}, {}
 
-        def gather_first(nb):
-            one[nb] = sb("one%d" % nb, [P, T], F32)
-            nc.vector.tensor_tensor(one[nb][:], y[nb][:].indirect(pos1_t[:]), gates[0][:], MULT)
-
-        def gather_second(nb):
-            two[nb] = sb("two%d" % nb, [P, T], F32)
-            nc.vector.tensor_tensor(two[nb][:], y[nb][:].indirect(pos2_t[:]), gates[1][:], MULT)
-
-        def add_turned(acc, parts):
-            for i, (j, part) in enumerate(parts):
-                nc.tensor.matmul(acc[:, j * P:(j + 1) * P], lhsT=part, rhs=ident[:],
-                                 start=(i == 0), stop=(i == len(parts) - 1), is_transpose=True)
-
-        def blocks(t):
-            return [(j, t[:, j * P:(j + 1) * P]) for j in range(TB)]
-
-        def sum_routed(nb, b):
-            acc = bank(b, [P, T])
-            add_turned(acc, blocks(one[nb]) + blocks(two[nb]))
-            summed[nb] = sb("summed%d" % nb, [P, T], F32)
-            act(summed[nb][:], acc[:])
-
-        def shared_turned(nb, b):
-            acc = bank(b, [P, T])
-            words, plane = w2_block(E, nb)
+        gate_banks = [bank(b, [P, T]) for b in (3, 0)]
+        for g in range(2):
             for j in range(TB):
-                cols = slice(j * P, (j + 1) * P)
-                nc.tensor.matmul_mx(
-                    out=acc[:, cols], lhsT=sc[:, cols].bitcast(FP8X4), lhsT_scale=ss[:, cols],
-                    rhs=words, rhs_scale=plane, start=True, stop=True,
-                )
-            yst[nb] = sb("yst%d" % nb, [P, T], F32)
-            act(yst[nb][:], acc[:])
+                nc.tensor.transpose(gate_banks[g][:, j * P:(j + 1) * P],
+                                    gate_cols[g][:, j:j + 1].to_broadcast([P, P]), ident[:])
 
-        def finish_turned(nb, b, parts):
-            back = bank(b, [P, T])
-            add_turned(back, blocks(parts[0][nb]) + blocks(parts[1][nb]))
-            o = sb("o%d" % nb, [P, T], F32)
-            act(o[:], back[:])
-            nc.scalar.dma_start(out=out[nb * P:(nb + 1) * P, :], in_=o[:])
+        def gather_gated(nb, g, name):
+            term[nb, g] = sb(name, [P, T], F32)
+            nc.vector.tensor_tensor(term[nb, g][:], y[nb][:].indirect(lists[g][:]), gates[g][:], MULT)
 
-        gather_first(0)
-        gather_second(0)
+        def gather_plain(nb, g, name):
+            term[nb, g] = sb(name, [P, T], F32)
+            nc.scalar.activation(term[nb, g][:], y[nb][:].indirect(lists[g][:]), COPY)
+
+        def gate_term(nb, g, name):
+            plain = term[nb, g]
+            term[nb, g] = sb(name, [P, T], F32)
+            nc.vector.tensor_tensor(term[nb, g][:], gate_banks[g][:], plain[:], MULT)
+
+        def add_shared(nb, g, b, name):
+            ys = bank(b, [P, T])
+            second(ys[:], E, nb, sc[:], ss[:])
+            part[nb] = sb(name, [P, T], F32)
+            nc.vector.tensor_tensor(part[nb][:], ys[:], term[nb, g][:], ADD)
+
+        def finish(nb, g, engine):
+            o = sb("gate1" if nb == 1 else "o%d" % nb, [P, T], F32)
+            engine.tensor_tensor(o[:], part[nb][:], term[nb, g][:], ADD)
+            nc.sync.dma_start(out=out[nb * P:(nb + 1) * P, :], in_=o[:])
+
+        gather_gated(0, 0, "term00")
+        gather_gated(0, 1, "term01")
         slots_out(1, 0, 4, act, 2)
         slots_out(1, 4, 8, act, 4)
-        gather_first(1)
-        for j, b in ((1, 2), (2, 4), (3, 2)):
+        for j, b in ((2, 5), (3, 1)):
             shared_first(j, b)
         sc = sb("shared_codes", [P, T], U32)
         ss = sb("shared_scales", [P, T], U8)
-        for g in range(2):
-            cols = slice(g * T // 2, (g + 1) * T // 2)
-            nc.vector.quantize_mx(out=sc[:, cols].bitcast(FP8X4), scales=ss[:, cols], in_=hqs[g][:])
-        gather_second(1)
+        nc.vector.quantize_mx(out=sc[:].bitcast(FP8X4), scales=ss[:], in_=hqs_all[:])
+        gather_plain(1, 0, "plain10")
+        gather_plain(1, 1, "plain11")
+        add_shared(0, 0, 2, "part0")
+        finish(0, 1, nc.gpsimd)
+        gate_term(1, 0, "term10")
+        add_shared(1, 0, 4, "part1")
+        gate_term(1, 1, "term00")
         slots_out(2, 0, 4, act, 5)
-        slots_out(2, 4, 8, act, 7)
-        gather_first(2)
-        gather_second(2)
-        sum_routed(0, 5)
+        slots_out(2, 4, 8, dve, 7)
         slots_out(3, 0, 4, act, 1)
         slots_out(3, 4, 8, act, 6)
-        gather_first(3)
-        sum_routed(1, 7)
-        shared_turned(0, 5)
-        shared_turned(1, 1)
-        shared_turned(2, 6)
-        ys = bank(3, [P, T])
-        second(ys[:], E, NB - 1, sc[:], ss[:])
-        part = sb("part", [P, T], F32)
-        nc.vector.tensor_tensor(part[:], ys[:], one[NB - 1][:], ADD)
-        finish_turned(0, 4, (summed, yst))
-        sum_routed(2, 5)
-        finish_turned(1, 2, (summed, yst))
-        finish_turned(2, 0, (yst, summed))
+        gather_plain(2, 0, "plain20")
+        gather_plain(2, 1, "plain21")
+        gather_gated(3, 1, "term10")
+        finish(1, 1, nc.gpsimd)
+        gate_term(2, 0, "plain11")
+        add_shared(2, 0, 5, "part2")
+        gate_term(2, 1, "plain20")
+        finish(2, 1, nc.gpsimd)
+        add_shared(3, 1, 7, "plain11")
+        last = sb("plain21", [P, T], F32)
         for i in range(2):
             cols = slice(i * T // 2, (i + 1) * T // 2)
-            last = sb("last%d" % i, [P, T // 2], F32)
-            nc.vector.tensor_tensor(last[:], y[NB - 1][:].indirect(pos2_t[:, i * 16:(i + 1) * 16]), gates[1][:, cols], MULT)
+            plain = sb("last_plain%d" % i, [P, T // 2], F32)
+            nc.scalar.activation(plain[:], y[NB - 1][:].indirect(pos1_t[:, i * 16:(i + 1) * 16]), COPY)
+            nc.vector.tensor_tensor(last[:, cols], gate_banks[0][:, cols], plain[:], MULT)
             o = sb("olast%d" % i, [P, T // 2], F32)
-            nc.vector.tensor_tensor(o[:], part[:, cols], last[:], ADD)
+            nc.vector.tensor_tensor(o[:], part[NB - 1][:, cols], last[:, cols], ADD)
             nc.sync.dma_start(out=out[(NB - 1) * P:NB * P, cols], in_=o[:])

@@ -288,31 +288,33 @@ def tile_moe_shr_mlp_silu_kernel(
         ss = sb("shared_scales", [P, T], U8)
         nc.vector.quantize_mx(out=sc[:].bitcast(FP8X4), scales=ss[:], in_=hqs_all[:])
         gather_plain(1, 0, "plain10")
+        plain = term[1, 0]
+        term[1, 0] = sb("hqs", [P, T], F32)
+        nc.gpsimd.tensor_tensor(term[1, 0][:], plain[:], gates[0][:], MULT)
         gather_plain(1, 1, "plain11")
-        add_shared(0, 0, 2, "part0")
-        finish(0, 1, nc.gpsimd)
-        gate_term(1, 0, "term10")
-        add_shared(1, 0, 4, "part1")
-        gate_term(1, 1, "term00")
-        slots_out(2, 0, 4, act, 5)
-        slots_out(2, 4, 8, dve, 7)
+        slots_out(2, 0, 4, dve, 5)
+        slots_out(2, 4, 8, act, 7)
         slots_out(3, 0, 4, act, 1)
         slots_out(3, 4, 8, act, 6)
+        add_shared(0, 0, 2, "part0")
+        finish(0, 1, nc.gpsimd)
+        add_shared(1, 0, 4, "part1")
+        gate_term(1, 1, "term00")
         gather_plain(2, 0, "plain20")
-        gather_plain(2, 1, "plain21")
-        gather_gated(3, 1, "term10")
+        gather_plain(3, 0, "plain30")
+        gather_gated(2, 1, "hqs")
         finish(1, 1, nc.gpsimd)
         gate_term(2, 0, "plain11")
-        add_shared(2, 0, 5, "part2")
-        gate_term(2, 1, "plain20")
-        finish(2, 1, nc.gpsimd)
-        add_shared(3, 1, 7, "plain11")
-        last = sb("plain21", [P, T], F32)
+        add_shared(2, 1, 5, "part2")
+        finish(2, 0, nc.gpsimd)
+        gate_term(3, 0, "plain20")
+        add_shared(3, 0, 7, "part3")
+        last = sb("hqs", [P, T], F32)
         for i in range(2):
             cols = slice(i * T // 2, (i + 1) * T // 2)
             plain = sb("last_plain%d" % i, [P, T // 2], F32)
-            nc.scalar.activation(plain[:], y[NB - 1][:].indirect(pos1_t[:, i * 16:(i + 1) * 16]), COPY)
-            nc.vector.tensor_tensor(last[:, cols], gate_banks[0][:, cols], plain[:], MULT)
+            nc.scalar.activation(plain[:], y[NB - 1][:].indirect(pos2_t[:, i * 16:(i + 1) * 16]), COPY)
+            nc.vector.tensor_tensor(last[:, cols], gate_banks[1][:, cols], plain[:], MULT)
             o = sb("olast%d" % i, [P, T // 2], F32)
             nc.vector.tensor_tensor(o[:], part[NB - 1][:, cols], last[:, cols], ADD)
             nc.sync.dma_start(out=out[(NB - 1) * P:NB * P, cols], in_=o[:])

@@ -159,14 +159,16 @@ def tile_moe_shr_mlp_silu_kernel(
         y = [sb("y%d" % nb, [P, S], F32) for nb in range(NB)]
         gw, gs = {}, {}
 
-        def gather_tokens(lo, hi):
-            entries = offs_t[:, lo * 8:hi * 8]
+        def gather_words(lo, hi):
             words = keep.tile([P, (hi - lo) * C], U32, name="gw", bufs=4, align_bytes=64)
-            scales = keep.tile([P, (hi - lo) * C], U8, name="gs", bufs=3, align_bytes=64)
-            nc.vector.tensor_copy(scales[:], xs[:].indirect(entries))
-            nc.vector.tensor_copy(words[:], xw[:].bitcast(U32).indirect(entries))
+            nc.vector.tensor_copy(words[:], xw[:].bitcast(U32).indirect(offs_t[:, lo * 8:hi * 8]))
             for e in range(lo, hi):
                 gw[e] = words[:, (e - lo) * C:(e - lo + 1) * C]
+
+        def gather_scales(lo, hi):
+            scales = keep.tile([P, (hi - lo) * C], U8, name="gs", bufs=3, align_bytes=64)
+            nc.vector.tensor_copy(scales[:], xs[:].indirect(offs_t[:, lo * 8:hi * 8]))
+            for e in range(lo, hi):
                 gs[e] = scales[:, (e - lo) * C:(e - lo + 1) * C]
 
         hcode, hscale = {}, {}
@@ -190,21 +192,21 @@ def tile_moe_shr_mlp_silu_kernel(
         def routed(e, b):
             h[e] = activate("h%d" % e, first_product(gw[e], gs[e], e, b))
 
-        unread = bank(7, [P, H])
-        for j in range(2):
-            nc.tensor.matmul_mx(
-                out=unread[:], lhsT=xw[:, j * P:(j + 1) * P].bitcast(FP8X4), lhsT_scale=xs[:, j * P:(j + 1) * P],
-                rhs=w1w[0].bitcast(FP4X4), rhs_scale=xs[:], start=True, stop=True,
-            )
-        gather_tokens(0, 1)
-        gather_tokens(1, 2)
+        gather_scales(0, 1)
+        gather_words(0, 1)
+        gather_scales(1, 2)
+        gather_words(1, 2)
+        gather_scales(2, 3)
         routed(0, 0)
-        gather_tokens(2, 4)
+        gather_words(2, 4)
+        gather_scales(3, 5)
         routed(1, 1)
-        gather_tokens(4, 6)
+        gather_words(4, 6)
+        gather_scales(5, 6)
         routed(2, 2)
         routed(3, 3)
-        gather_tokens(6, 8)
+        gather_scales(6, 8)
+        gather_words(6, 8)
         routed(4, 0)
         routed(5, 1)
 
@@ -221,13 +223,13 @@ def tile_moe_shr_mlp_silu_kernel(
                                  a[:].rearrange("p t s -> p s t"), SILU)
 
         turn([h[0], h[1]], hq03[:, 0:2 * W], dve, 2)
-        w1p = sb("h0", [P, 2 * H], U8)
-        w1ps = sb("h1", [P, H], U8)
+        turn([h[2], h[3]], hq03[:, 2 * W:4 * W], dve, 4)
+        w1p = sb("h2", [P, 2 * H], U8)
+        w1ps = sb("h3", [P, H], U8)
         nc.gpsimd.tensor_copy(w1p[:].bitcast(U16).rearrange("p (t m) -> p t m", t=4),
                               w1w[E].bitcast(U16).rearrange("p (m t) -> p t m", t=4))
         nc.gpsimd.tensor_copy(w1ps[:].rearrange("p (t m) -> p t m", t=4), w1_plane(E).rearrange("p (m t) -> p t m", t=4))
 
-        turn([h[2], h[3]], hq03[:, 2 * W:4 * W], dve, 4)
         routed(6, 3)
         routed(7, 0)
         turn([h[4], h[5]], hq45[:], dve, 5)

@@ -192,7 +192,16 @@ def tile_moe_shr_mlp_silu_kernel(
         def routed(e, b):
             h[e] = activate("h%d" % e, first_product(gw[e], gs[e], e, b))
 
+        shared_xs = sb("shared_xs", [P, T], U8)
+        dve(shared_xs[:].bitcast(I32), xs[:].bitcast(I32))
         gather_scales(0, 1)
+        shared_xw = sb("shared_xw", [P, P], I32)
+        dve(shared_xw[:], xw[:, 0:P])
+        unread = bank(7, [P, H])
+        nc.tensor.matmul_mx(
+            out=unread[:], lhsT=shared_xw[:].bitcast(FP8X4), lhsT_scale=shared_xs[:, 0:P],
+            rhs=w1w[0].bitcast(FP4X4), rhs_scale=shared_xs[:], start=True, stop=True,
+        )
         gather_words(0, 1)
         gather_scales(1, 2)
         gather_words(1, 2)
@@ -217,7 +226,8 @@ def tile_moe_shr_mlp_silu_kernel(
                 nc.tensor.matmul_mx(
                     out=a[:, t, :], lhsT=w1p[:, t * 2 * P:(t + 1) * 2 * P].bitcast(FP4X4),
                     lhsT_scale=w1ps[:, t * P:(t + 1) * P],
-                    rhs=xw[:, cols].bitcast(FP8X4), rhs_scale=xs[:, cols], start=True, stop=True,
+                    rhs=(shared_xw[:] if j == 0 else xw[:, cols]).bitcast(FP8X4), rhs_scale=shared_xs[:, cols],
+                    start=True, stop=True,
                 )
             nc.scalar.activation(hqs[j // 2][:, (j % 2) * W:(j % 2 + 1) * W].rearrange("p (s t) -> p s t", t=4),
                                  a[:].rearrange("p t s -> p s t"), SILU)

@@ -8,6 +8,10 @@ S = E * C
 P = 128
 NB = N // P
 TB = T // P
+HALF = N // 2
+FIRST = 2
+W = 4 * C
+LIST_COLS = C // 16
 
 FLOPS = 2 * (S + T) * (K * H + H * N)
 BYTES = (K * T + K * T // 32) + 2 * (E + 1) * (K * H // 2 + K * H // 32) + 2 * T * 4 + 2 * (S + 2 * T) + N * T * 4
@@ -45,15 +49,13 @@ def tile_moe_shr_mlp_silu_kernel(
         pos2_t = keep.tile([P, T // 16], U16, name="pos2_t")
         xw = sb("xw", [P, T], I32)
         xs = sb("xs", [P, T], U8)
-        FIRST = 2
         w1s_a = sb("w1s_a", [P, FIRST * H], U8)
         w1s_b = sb("w1s_b", [P, (E + 1 - FIRST) * H], U8)
-        HALF = N // 2
         w2s = [sb("w2s%d" % half, [P, (E + 1) * HALF], U8) for half in range(2)]
         ident = sb("ident", [P, P], F32)
 
         def words_tile(name, words, lo, hi, queue):
-            t = sb(name, [P, hi - lo, 1024], U8)
+            t = sb(name, [P, hi - lo, 2 * H], U8)
             queue.dma_start(out=t[:].bitcast(I32), in_=words[lo:hi, 0].bitcast(I32).rearrange("e p c -> p e c"))
             return [t[:, e, :] for e in range(hi - lo)]
 
@@ -71,10 +73,13 @@ def tile_moe_shr_mlp_silu_kernel(
         make_identity(nc, ident[:])
 
         nc.sync.dma_start(offs_t[:], offs)
-        w1w = words_tile("w1w_0", w1_words, 0, 1, nc.sync) + next_words
+        all_words = x_words[0].rearrange("p t r -> p (t r)").bitcast(I32)
+        shared_xw = sb("shared_xw", [P, P], I32)
+        nc.sync.dma_start(out=shared_xw[:], in_=all_words[:, 0:P])
         for r in range(4):
             scale_rows(xs, x_scales, r)
-        nc.sync.dma_start(out=xw[:], in_=x_words[0].rearrange("p t r -> p (t r)").bitcast(I32))
+        w1w = words_tile("w1w_0", w1_words, 0, 1, nc.sync) + next_words
+        nc.sync.dma_start(out=xw[:], in_=all_words)
         for r in range(4):
             scale_rows(w1s_a, w1_scales[0:FIRST, 0], r)
         for r in range(4):
@@ -161,13 +166,13 @@ def tile_moe_shr_mlp_silu_kernel(
 
         def gather_words(lo, hi):
             words = keep.tile([P, (hi - lo) * C], U32, name="gw", bufs=4, align_bytes=64)
-            nc.vector.tensor_copy(words[:], xw[:].bitcast(U32).indirect(offs_t[:, lo * 8:hi * 8]))
+            nc.vector.tensor_copy(words[:], xw[:].bitcast(U32).indirect(offs_t[:, lo * LIST_COLS:hi * LIST_COLS]))
             for e in range(lo, hi):
                 gw[e] = words[:, (e - lo) * C:(e - lo + 1) * C]
 
         def gather_scales(lo, hi):
             scales = keep.tile([P, (hi - lo) * C], U8, name="gs", bufs=3, align_bytes=64)
-            nc.vector.tensor_copy(scales[:], xs[:].indirect(offs_t[:, lo * 8:hi * 8]))
+            nc.vector.tensor_copy(scales[:], xs[:].indirect(offs_t[:, lo * LIST_COLS:hi * LIST_COLS]))
             for e in range(lo, hi):
                 gs[e] = scales[:, (e - lo) * C:(e - lo + 1) * C]
 
@@ -185,7 +190,6 @@ def tile_moe_shr_mlp_silu_kernel(
                 second(acc[:, (e - lo) * C:(e - lo + 1) * C], e, nb, hcode[e], hscale[e])
             copy(y[nb][:, lo * C:hi * C], acc[:])
 
-        W = 4 * C
         hq03, hq45, hq6, hq7 = (sb(name, [P, n * W], BF16) for name, n in (("hq03", 4), ("hq45", 2), ("hq6", 1), ("hq7", 1)))
         h = {}
 
@@ -195,23 +199,21 @@ def tile_moe_shr_mlp_silu_kernel(
         shared_xs = sb("shared_xs", [P, T], U8)
         dve(shared_xs[:].bitcast(I32), xs[:].bitcast(I32))
         gather_scales(0, 1)
-        shared_xw = sb("shared_xw", [P, P], I32)
-        dve(shared_xw[:], xw[:, 0:P])
-        unread = bank(7, [P, H])
-        nc.tensor.matmul_mx(
-            out=unread[:], lhsT=shared_xw[:].bitcast(FP8X4), lhsT_scale=shared_xs[:, 0:P],
-            rhs=w1w[0].bitcast(FP4X4), rhs_scale=shared_xs[:], start=True, stop=True,
-        )
+        for b in (6, 7):
+            unread = bank(b, [P, H])
+            nc.tensor.matmul_mx(
+                out=unread[:], lhsT=shared_xw[:].bitcast(FP8X4), lhsT_scale=shared_xs[:, 0:P],
+                rhs=w1w[0].bitcast(FP4X4), rhs_scale=shared_xs[:], start=True, stop=True,
+            )
         gather_words(0, 1)
         gather_scales(1, 2)
         gather_words(1, 2)
-        gather_scales(2, 3)
         routed(0, 0)
+        gather_scales(2, 4)
         gather_words(2, 4)
-        gather_scales(3, 5)
         routed(1, 1)
+        gather_scales(4, 6)
         gather_words(4, 6)
-        gather_scales(5, 6)
         routed(2, 2)
         routed(3, 3)
         gather_scales(6, 8)
@@ -221,32 +223,31 @@ def tile_moe_shr_mlp_silu_kernel(
 
         def shared_first(j, b):
             cols = slice(j * P, (j + 1) * P)
+            words = shared_xw[:] if j == 0 else xw[:, cols]
             a = bank(b, [P, 4, P])
             for t in range(4):
                 nc.tensor.matmul_mx(
                     out=a[:, t, :], lhsT=w1p[:, t * 2 * P:(t + 1) * 2 * P].bitcast(FP4X4),
                     lhsT_scale=w1ps[:, t * P:(t + 1) * P],
-                    rhs=(shared_xw[:] if j == 0 else xw[:, cols]).bitcast(FP8X4), rhs_scale=shared_xs[:, cols],
-                    start=True, stop=True,
+                    rhs=words.bitcast(FP8X4), rhs_scale=shared_xs[:, cols], start=True, stop=True,
                 )
-            nc.scalar.activation(hqs[j // 2][:, (j % 2) * W:(j % 2 + 1) * W].rearrange("p (s t) -> p s t", t=4),
+            nc.scalar.activation(hqs[:, j * W:(j + 1) * W].rearrange("p (s t) -> p s t", t=4),
                                  a[:].rearrange("p t s -> p s t"), SILU)
 
         turn([h[0], h[1]], hq03[:, 0:2 * W], dve, 2)
-        turn([h[2], h[3]], hq03[:, 2 * W:4 * W], dve, 4)
-        w1p = sb("h2", [P, 2 * H], U8)
-        w1ps = sb("h3", [P, H], U8)
+        w1p = sb("h0", [P, 2 * H], U8)
+        w1ps = sb("h1", [P, H], U8)
         nc.gpsimd.tensor_copy(w1p[:].bitcast(U16).rearrange("p (t m) -> p t m", t=4),
                               w1w[E].bitcast(U16).rearrange("p (m t) -> p t m", t=4))
         nc.gpsimd.tensor_copy(w1ps[:].rearrange("p (t m) -> p t m", t=4), w1_plane(E).rearrange("p (m t) -> p t m", t=4))
+        turn([h[2], h[3]], hq03[:, 2 * W:4 * W], dve, 4)
 
         routed(6, 3)
         routed(7, 0)
         turn([h[4], h[5]], hq45[:], dve, 5)
-        turn([h[6]], hq6[:], dve, 6)
+        turn([h[6]], hq6[:], act, 6)
         turn([h[7]], hq7[:], act, 7)
-        hqs_all = sb("hqs", [P, 4 * W], BF16)
-        hqs = [hqs_all[:, 0:2 * W], hqs_all[:, 2 * W:4 * W]]
+        hqs = sb("hqs", [P, TB * W], BF16)
         shared_first(0, 3)
         shared_first(1, 0)
         quantize_experts(0, 4, hq03[:])
@@ -285,9 +286,9 @@ def tile_moe_shr_mlp_silu_kernel(
             part[nb] = sb(name, [P, T], F32)
             nc.vector.tensor_tensor(part[nb][:], ys[:], term[nb, g][:], ADD)
 
-        def finish(nb, g, engine):
-            o = sb("gate1" if nb == 1 else "o%d" % nb, [P, T], F32)
-            engine.tensor_tensor(o[:], part[nb][:], term[nb, g][:], ADD)
+        def finish(nb, g, name):
+            o = sb(name, [P, T], F32)
+            nc.gpsimd.tensor_tensor(o[:], part[nb][:], term[nb, g][:], ADD)
             nc.sync.dma_start(out=out[nb * P:(nb + 1) * P, :], in_=o[:])
 
         gather_gated(0, 0, "term00")
@@ -298,34 +299,34 @@ def tile_moe_shr_mlp_silu_kernel(
             shared_first(j, b)
         sc = sb("shared_codes", [P, T], U32)
         ss = sb("shared_scales", [P, T], U8)
-        nc.vector.quantize_mx(out=sc[:].bitcast(FP8X4), scales=ss[:], in_=hqs_all[:])
+        nc.vector.quantize_mx(out=sc[:].bitcast(FP8X4), scales=ss[:], in_=hqs[:])
         gather_plain(1, 0, "plain10")
-        plain = term[1, 0]
+        plain10 = term[1, 0]
         term[1, 0] = sb("hqs", [P, T], F32)
-        nc.gpsimd.tensor_tensor(term[1, 0][:], plain[:], gates[0][:], MULT)
+        nc.gpsimd.tensor_tensor(term[1, 0][:], plain10[:], gates[0][:], MULT)
         gather_plain(1, 1, "plain11")
         slots_out(2, 0, 4, dve, 5)
         slots_out(2, 4, 8, act, 7)
         slots_out(3, 0, 4, act, 1)
         slots_out(3, 4, 8, act, 6)
         add_shared(0, 0, 2, "part0")
-        finish(0, 1, nc.gpsimd)
+        finish(0, 1, "o0")
         add_shared(1, 0, 4, "part1")
         gate_term(1, 1, "term00")
         gather_plain(2, 0, "plain20")
         gather_plain(3, 0, "plain30")
         gather_gated(2, 1, "hqs")
-        finish(1, 1, nc.gpsimd)
+        finish(1, 1, "gate1")
         gate_term(2, 0, "plain11")
         add_shared(2, 1, 5, "part2")
-        finish(2, 0, nc.gpsimd)
+        finish(2, 0, "o2")
         gate_term(3, 0, "plain20")
         add_shared(3, 0, 7, "part3")
         last = sb("hqs", [P, T], F32)
         for i in range(2):
             cols = slice(i * T // 2, (i + 1) * T // 2)
             plain = sb("last_plain%d" % i, [P, T // 2], F32)
-            nc.scalar.activation(plain[:], y[NB - 1][:].indirect(pos2_t[:, i * 16:(i + 1) * 16]), COPY)
+            nc.scalar.activation(plain[:], y[NB - 1][:].indirect(pos2_t[:, cols.start // 16:cols.stop // 16]), COPY)
             nc.vector.tensor_tensor(last[:, cols], gate_banks[1][:, cols], plain[:], MULT)
             o = sb("olast%d" % i, [P, T // 2], F32)
             nc.vector.tensor_tensor(o[:], part[NB - 1][:, cols], last[:, cols], ADD)

@@ -291,38 +291,44 @@ def tile_moe_shr_mlp_silu_kernel(
             nc.gpsimd.tensor_tensor(o[:], part[nb][:], term[nb, g][:], ADD)
             nc.sync.dma_start(out=out[nb * P:(nb + 1) * P, :], in_=o[:])
 
+        def store(nb, o):
+            nc.sync.dma_start(out=out[nb * P:(nb + 1) * P, :], in_=o[:])
+
         gather_gated(0, 0, "term00")
         gather_gated(0, 1, "term01")
         slots_out(1, 0, 4, act, 2)
         slots_out(1, 4, 8, act, 4)
+        gather_gated(1, 1, "term11")
         for j, b in ((2, 5), (3, 1)):
             shared_first(j, b)
         sc = sb("shared_codes", [P, T], U32)
         ss = sb("shared_scales", [P, T], U8)
         nc.vector.quantize_mx(out=sc[:].bitcast(FP8X4), scales=ss[:], in_=hqs[:])
         gather_plain(1, 0, "plain10")
-        plain10 = term[1, 0]
-        term[1, 0] = sb("hqs", [P, T], F32)
-        nc.gpsimd.tensor_tensor(term[1, 0][:], plain10[:], gates[0][:], MULT)
-        gather_plain(1, 1, "plain11")
-        slots_out(2, 0, 4, dve, 5)
-        slots_out(2, 4, 8, act, 7)
-        slots_out(3, 0, 4, act, 1)
-        slots_out(3, 4, 8, act, 6)
-        add_shared(0, 0, 2, "part0")
-        finish(0, 1, "o0")
-        add_shared(1, 0, 4, "part1")
-        gate_term(1, 1, "term00")
+        sum0 = sb("hqs", [P, T], F32)
+        nc.gpsimd.tensor_tensor(sum0[:], term[0, 0][:], term[0, 1][:], ADD)
+        term[0, 0] = sum0
+        slots_out(2, 0, 4, act, 7)
+        slots_out(2, 4, 8, act, 6)
+        gate_term(1, 0, "term10")
+        slots_out(3, 0, 4, dve, 1)
         gather_plain(2, 0, "plain20")
+        slots_out(3, 4, 8, act, 5)
+        add_shared(1, 0, 4, "part1")
+        finish(1, 1, "o1")
+        add_shared(0, 0, 2, "part0")
+        store(0, part[0])
+        gather_plain(2, 1, "plain21")
+        gate_term(2, 0, "term20")
+        plain21 = term[2, 1]
+        term[2, 1] = sb("term21", [P, T], F32)
+        nc.gpsimd.tensor_tensor(term[2, 1][:], plain21[:], gates[1][:], MULT)
         gather_plain(3, 0, "plain30")
-        gather_gated(2, 1, "hqs")
-        finish(1, 1, "gate1")
-        gate_term(2, 0, "plain11")
-        add_shared(2, 1, 5, "part2")
-        finish(2, 0, "o2")
-        gate_term(3, 0, "plain20")
-        add_shared(3, 0, 7, "part3")
-        last = sb("hqs", [P, T], F32)
+        add_shared(2, 0, 7, "part2")
+        finish(2, 1, "o2")
+        gate_term(3, 0, "term30")
+        add_shared(3, 0, 6, "part3")
+        last = sb("last", [P, T], F32)
         for i in range(2):
             cols = slice(i * T // 2, (i + 1) * T // 2)
             plain = sb("last_plain%d" % i, [P, T // 2], F32)

from contextlib import ExitStack

import concourse.mybir as mybir
from concourse.masks import make_identity

K, T, E, C, H, N = 512, 512, 8, 128, 512, 512
S = E * C
P = 128
NB = N // P
TB = T // P
HALF = N // 2
FIRST = 2
W = 4 * C
LIST_COLS = C // 16

FLOPS = 2 * (S + T) * (K * H + H * N)
BYTES = (K * T + K * T // 32) + 2 * (E + 1) * (K * H // 2 + K * H // 32) + 2 * T * 4 + 2 * (S + 2 * T) + N * T * 4

F32 = mybir.dt.float32
BF16 = mybir.dt.bfloat16
I32 = mybir.dt.int32
U32 = mybir.dt.uint32
U16 = mybir.dt.uint16
U8 = mybir.dt.uint8
FP8X4 = mybir.dt.float8_e4m3fn_x4
FP4X4 = mybir.dt.float4_e2m1fn_x4
MULT = mybir.AluOpType.mult
ADD = mybir.AluOpType.add
SILU = mybir.ActivationFunctionType.Silu
COPY = mybir.ActivationFunctionType.Copy


def tile_moe_shr_mlp_silu_kernel(
    tc, x_words, x_scales, w1_words, w1_scales, w2_words, w2_scales, gate, offs, pos1, pos2, out
):
    nc = tc.nc
    with ExitStack() as ctx:
        keep = ctx.enter_context(tc.tile_pool(name="keep", bufs=1))
        psum = ctx.enter_context(tc.psum_pool(name="psum", bufs=1))

        def bank(i, shape):
            return psum.tile(shape, F32, name="bank%d" % i)

        def sb(name, shape, dtype):
            return keep.tile(shape, dtype, name=name, align_bytes=64)

        offs_t = keep.tile([P, S // 16], U16, name="offs_t")
        pos1_t = keep.tile([P, T // 16], U16, name="pos1_t")
        pos2_t = keep.tile([P, T // 16], U16, name="pos2_t")
        xw = sb("xw", [P, T], I32)
        xs = sb("xs", [P, T], U8)
        w1s_a = sb("w1s_a", [P, FIRST * H], U8)
        w1s_b = sb("w1s_b", [P, (E + 1 - FIRST) * H], U8)
        w2s = [sb("w2s%d" % half, [P, (E + 1) * HALF], U8) for half in range(2)]
        ident = sb("ident", [P, P], F32)

        def words_tile(name, words, lo, hi, queue):
            t = sb(name, [P, hi - lo, 2 * H], U8)
            queue.dma_start(out=t[:].bitcast(I32), in_=words[lo:hi, 0].bitcast(I32).rearrange("e p c -> p e c"))
            return [t[:, e, :] for e in range(hi - lo)]

        def scale_rows(plane, rows, r):
            src = rows.bitcast(I32).rearrange("e (q r) c -> r q e c", r=4)
            view = plane[:].bitcast(I32)
            nc.sync.dma_start(out=view[r:P:32, :].rearrange("q (e c) -> q e c", e=rows.shape[0]), in_=src[r])

        next_words = words_tile("w1w_13", w1_words, 1, 4, nc.gpsimd)
        later_words = w1s_b[:].bitcast(I32)
        odd = later_words.shape[1] // 2 + 1
        for words in (xs[:].bitcast(I32), w1s_a[:].bitcast(I32), later_words[:, 0:odd], later_words[:, odd:],
                      w2s[0][:].bitcast(I32), w2s[1][:].bitcast(I32)):
            nc.vector.memset(words, 0)
        make_identity(nc, ident[:])

        nc.sync.dma_start(offs_t[:], offs)
        all_words = x_words[0].rearrange("p t r -> p (t r)").bitcast(I32)
        shared_xw = sb("shared_xw", [P, P], I32)
        nc.sync.dma_start(out=shared_xw[:], in_=all_words[:, 0:P])
        for r in range(4):
            scale_rows(xs, x_scales, r)
        w1w = words_tile("w1w_0", w1_words, 0, 1, nc.sync) + next_words
        nc.sync.dma_start(out=xw[:], in_=all_words)
        for r in range(4):
            scale_rows(w1s_a, w1_scales[0:FIRST, 0], r)
        for r in range(4):
            scale_rows(w1s_b, w1_scales[FIRST:, 0], r)
        w1w = w1w + words_tile("w1w_45", w1_words, 4, 6, nc.sync) + words_tile("w1w_68", w1_words, 6, 9, nc.sync)
        for r in range(4):
            scale_rows(w2s[0], w2_scales[:, 0, :, 0:HALF], r)

        def w2_columns(name, lo, hi):
            t = sb(name, [P, E, 2 * (hi - lo)], U8)
            src = w2_words[0:E, 0, :, 2 * lo:2 * hi].bitcast(I32).rearrange("e p c -> p e c")
            nc.sync.dma_start(out=t[:].bitcast(I32), in_=src)
            return [t[:, :, 2 * c:2 * (c + P)] for c in range(0, hi - lo, P)]

        gates = [sb("gate%d" % g, [P, T], F32) for g in range(2)]
        w2w = w2_columns("w2w_01", 0, HALF)
        nc.sync.dma_start(pos1_t[:], pos1)
        nc.sync.dma_start(out=gates[0][:], in_=gate[0, 0:P, :])
        nc.sync.dma_start(pos2_t[:], pos2)
        nc.sync.dma_start(out=gates[1][:], in_=gate[1, 0:P, :])
        gate_cols = [sb("gate_cols%d" % g, [P, TB], F32) for g in range(2)]
        with nc.allow_non_contiguous_dma(reason="one gate value a partition"):
            for g in range(2):
                nc.sync.dma_start(out=gate_cols[g][:], in_=gate[g, 0, :].rearrange("(j p) -> p j", p=P))
        for r in range(4):
            scale_rows(w2s[1], w2_scales[:, 0, :, HALF:N], r)
        w2w = w2w + w2_columns("w2w_23", HALF, N)
        w2_shared = words_tile("w2w_shared", w2_words, E, E + 1, nc.sync)[0]

        def w2_block(e, nb):
            words = w2_shared[:, nb * 2 * P:(nb + 1) * 2 * P] if e == E else w2w[nb][:, e, :]
            return words.bitcast(FP4X4), w2s[nb // 2][:, e * HALF + (nb % 2) * P:e * HALF + (nb % 2 + 1) * P]

        def w1_plane(e):
            if e < FIRST:
                return w1s_a[:, e * H:(e + 1) * H]
            return w1s_b[:, (e - FIRST) * H:(e - FIRST + 1) * H]

        act, dve = nc.scalar.copy, nc.vector.tensor_copy

        def first_product(words, scales, e, b):
            a = bank(b, [P, H])
            nc.tensor.matmul_mx(
                out=a[:], lhsT=words.bitcast(FP8X4), lhsT_scale=scales,
                rhs=w1w[e].bitcast(FP4X4), rhs_scale=w1_plane(e), start=True, stop=True,
            )
            return a

        def activate(name, a):
            h = sb(name, [P, H], BF16)
            nc.scalar.activation(
                h[:].rearrange("s (u p e) -> s u p e", u=2, e=2),
                a[:].rearrange("s (p u e) -> s u p e", u=2, e=2), SILU,
            )
            return h

        def turn(hb, hq, copy, b):
            n = len(hb)
            turned = bank(b, [P, 2 * n, P])
            for c in range(n):
                pairs = hb[c][:].bitcast(F32)
                for u in range(2):
                    nc.tensor.transpose(turned[:, 2 * c + u, :], pairs[:, u * P:(u + 1) * P], ident[:])
            copy(
                hq.bitcast(F32).rearrange("p (c s u) -> p c s u", c=n, u=2),
                turned[:].rearrange("p (c u) s -> p c s u", u=2),
            )

        def quantize(name, hq, blocks):
            codes = sb(name + "_codes", [P, blocks * P], U32)
            scales = sb(name + "_scales", [P, blocks * P], U8)
            nc.vector.quantize_mx(out=codes[:].bitcast(FP8X4), scales=scales[:], in_=hq)
            return codes, scales

        def second(acc, e, nb, codes, scales):
            words, plane = w2_block(e, nb)
            nc.tensor.matmul_mx(
                out=acc, lhsT=words, lhsT_scale=plane,
                rhs=codes.bitcast(FP8X4), rhs_scale=scales, start=True, stop=True,
            )

        y = [sb("y%d" % nb, [P, S], F32) for nb in range(NB)]
        gw, gs = {}, {}

        def gather_words(lo, hi):
            words = keep.tile([P, (hi - lo) * C], U32, name="gw", bufs=4, align_bytes=64)
            nc.vector.tensor_copy(words[:], xw[:].bitcast(U32).indirect(offs_t[:, lo * LIST_COLS:hi * LIST_COLS]))
            for e in range(lo, hi):
                gw[e] = words[:, (e - lo) * C:(e - lo + 1) * C]

        def gather_scales(lo, hi):
            scales = keep.tile([P, (hi - lo) * C], U8, name="gs", bufs=3, align_bytes=64)
            nc.vector.tensor_copy(scales[:], xs[:].indirect(offs_t[:, lo * LIST_COLS:hi * LIST_COLS]))
            for e in range(lo, hi):
                gs[e] = scales[:, (e - lo) * C:(e - lo + 1) * C]

        hcode, hscale = {}, {}

        def quantize_experts(lo, hi, hq):
            codes, scales = quantize("q%d" % lo, hq, hi - lo)
            for e in range(lo, hi):
                hcode[e] = codes[:, (e - lo) * C:(e - lo + 1) * C]
                hscale[e] = scales[:, (e - lo) * C:(e - lo + 1) * C]

        def slots_out(nb, lo, hi, copy, b):
            acc = bank(b, [P, (hi - lo) * C])
            for e in range(lo, hi):
                second(acc[:, (e - lo) * C:(e - lo + 1) * C], e, nb, hcode[e], hscale[e])
            copy(y[nb][:, lo * C:hi * C], acc[:])

        hq03, hq45, hq6, hq7 = (sb(name, [P, n * W], BF16) for name, n in (("hq03", 4), ("hq45", 2), ("hq6", 1), ("hq7", 1)))
        h = {}

        def routed(e, b):
            h[e] = activate("h%d" % e, first_product(gw[e], gs[e], e, b))

        shared_xs = sb("shared_xs", [P, T], U8)
        dve(shared_xs[:].bitcast(I32), xs[:].bitcast(I32))
        gather_scales(0, 1)
        for b in (6, 7):
            unread = bank(b, [P, H])
            nc.tensor.matmul_mx(
                out=unread[:], lhsT=shared_xw[:].bitcast(FP8X4), lhsT_scale=shared_xs[:, 0:P],
                rhs=w1w[0].bitcast(FP4X4), rhs_scale=shared_xs[:], start=True, stop=True,
            )
        gather_words(0, 1)
        gather_scales(1, 2)
        gather_words(1, 2)
        routed(0, 0)
        gather_scales(2, 4)
        gather_words(2, 4)
        routed(1, 1)
        gather_scales(4, 6)
        gather_words(4, 6)
        routed(2, 2)
        routed(3, 3)
        gather_scales(6, 8)
        gather_words(6, 8)
        routed(4, 0)
        routed(5, 1)

        def shared_first(j, b):
            cols = slice(j * P, (j + 1) * P)
            words = shared_xw[:] if j == 0 else xw[:, cols]
            a = bank(b, [P, 4, P])
            for t in range(4):
                nc.tensor.matmul_mx(
                    out=a[:, t, :], lhsT=w1p[:, t * 2 * P:(t + 1) * 2 * P].bitcast(FP4X4),
                    lhsT_scale=w1ps[:, t * P:(t + 1) * P],
                    rhs=words.bitcast(FP8X4), rhs_scale=shared_xs[:, cols], start=True, stop=True,
                )
            nc.scalar.activation(hqs[:, j * W:(j + 1) * W].rearrange("p (s t) -> p s t", t=4),
                                 a[:].rearrange("p t s -> p s t"), SILU)

        turn([h[0], h[1]], hq03[:, 0:2 * W], dve, 2)
        w1p = sb("h0", [P, 2 * H], U8)
        w1ps = sb("h1", [P, H], U8)
        nc.gpsimd.tensor_copy(w1p[:].bitcast(U16).rearrange("p (t m) -> p t m", t=4),
                              w1w[E].bitcast(U16).rearrange("p (m t) -> p t m", t=4))
        nc.gpsimd.tensor_copy(w1ps[:].rearrange("p (t m) -> p t m", t=4), w1_plane(E).rearrange("p (m t) -> p t m", t=4))
        turn([h[2], h[3]], hq03[:, 2 * W:4 * W], dve, 4)

        routed(6, 3)
        routed(7, 0)
        turn([h[4], h[5]], hq45[:], dve, 5)
        turn([h[6]], hq6[:], act, 6)
        turn([h[7]], hq7[:], act, 7)
        hqs = sb("hqs", [P, TB * W], BF16)
        shared_first(0, 3)
        shared_first(1, 0)
        quantize_experts(0, 4, hq03[:])
        quantize_experts(4, 6, hq45[:])
        quantize_experts(6, 7, hq6[:])
        quantize_experts(7, 8, hq7[:])
        slots_out(0, 0, 4, dve, 1)
        slots_out(0, 4, 6, act, 5)
        slots_out(0, 6, 8, dve, 6)

        lists = (pos1_t, pos2_t)
        term, part = {}, {}

        gate_banks = [bank(b, [P, T]) for b in (3, 0)]
        for g in range(2):
            for j in range(TB):
                nc.tensor.transpose(gate_banks[g][:, j * P:(j + 1) * P],
                                    gate_cols[g][:, j:j + 1].to_broadcast([P, P]), ident[:])

        def gather_gated(nb, g, name):
            term[nb, g] = sb(name, [P, T], F32)
            nc.vector.tensor_tensor(term[nb, g][:], y[nb][:].indirect(lists[g][:]), gates[g][:], MULT)

        def gather_plain(nb, g, name):
            term[nb, g] = sb(name, [P, T], F32)
            nc.scalar.activation(term[nb, g][:], y[nb][:].indirect(lists[g][:]), COPY)

        def gate_term(nb, g, name):
            plain = term[nb, g]
            term[nb, g] = sb(name, [P, T], F32)
            nc.vector.tensor_tensor(term[nb, g][:], gate_banks[g][:], plain[:], MULT)

        def add_shared(nb, g, b, name):
            ys = bank(b, [P, T])
            second(ys[:], E, nb, sc[:], ss[:])
            part[nb] = sb(name, [P, T], F32)
            nc.vector.tensor_tensor(part[nb][:], ys[:], term[nb, g][:], ADD)

        def finish(nb, g, name):
            o = sb(name, [P, T], F32)
            nc.gpsimd.tensor_tensor(o[:], part[nb][:], term[nb, g][:], ADD)
            nc.sync.dma_start(out=out[nb * P:(nb + 1) * P, :], in_=o[:])

        def store(nb, o):
            nc.sync.dma_start(out=out[nb * P:(nb + 1) * P, :], in_=o[:])

        gather_gated(0, 0, "term00")
        gather_gated(0, 1, "term01")
        slots_out(1, 0, 4, act, 2)
        slots_out(1, 4, 8, act, 4)
        gather_gated(1, 1, "term11")
        for j, b in ((2, 5), (3, 1)):
            shared_first(j, b)
        sc = sb("shared_codes", [P, T], U32)
        ss = sb("shared_scales", [P, T], U8)
        nc.vector.quantize_mx(out=sc[:].bitcast(FP8X4), scales=ss[:], in_=hqs[:])
        gather_plain(1, 0, "plain10")
        sum0 = sb("hqs", [P, T], F32)
        nc.gpsimd.tensor_tensor(sum0[:], term[0, 0][:], term[0, 1][:], ADD)
        term[0, 0] = sum0
        slots_out(2, 0, 4, act, 7)
        slots_out(2, 4, 8, act, 6)
        gate_term(1, 0, "term10")
        slots_out(3, 0, 4, dve, 1)
        gather_plain(2, 0, "plain20")
        slots_out(3, 4, 8, act, 5)
        add_shared(1, 0, 4, "part1")
        finish(1, 1, "o1")
        add_shared(0, 0, 2, "part0")
        store(0, part[0])
        gather_plain(2, 1, "plain21")
        gate_term(2, 0, "term20")
        plain21 = term[2, 1]
        term[2, 1] = sb("term21", [P, T], F32)
        nc.gpsimd.tensor_tensor(term[2, 1][:], plain21[:], gates[1][:], MULT)
        gather_plain(3, 0, "plain30")
        add_shared(2, 0, 7, "part2")
        finish(2, 1, "o2")
        gate_term(3, 0, "term30")
        add_shared(3, 0, 6, "part3")
        last = sb("last", [P, T], F32)
        for i in range(2):
            cols = slice(i * T // 2, (i + 1) * T // 2)
            plain = sb("last_plain%d" % i, [P, T // 2], F32)
            nc.scalar.activation(plain[:], y[NB - 1][:].indirect(pos2_t[:, cols.start // 16:cols.stop // 16]), COPY)
            nc.vector.tensor_tensor(last[:, cols], gate_banks[1][:, cols], plain[:], MULT)
            o = sb("olast%d" % i, [P, T // 2], F32)
            nc.vector.tensor_tensor(o[:], part[NB - 1][:, cols], last[:, cols], ADD)
            nc.sync.dma_start(out=out[(NB - 1) * P:NB * P, cols], in_=o[:])
